import numpy as np
import ml_dtypes


def mxq(x, axis, fmt="e4m3"):
    dtype, down = {"e4m3": (ml_dtypes.float8_e4m3fn, 7), "e5m2": (ml_dtypes.float8_e5m2, 14)}[fmt]
    v = np.moveaxis(np.asarray(x, np.float32).astype(ml_dtypes.bfloat16).astype(np.float64), axis, -1)
    blocks = v.reshape(v.shape[:-1] + (-1, 32))
    amax = np.abs(blocks).max(-1, keepdims=True)
    byte = np.maximum(np.where(amax > 0, np.frexp(amax)[1] - 1 + 127, 0) - down, 1)
    scale = np.exp2(byte - 127.0)
    codes = (blocks / scale).astype(np.float32).astype(dtype).astype(np.float64)
    return np.moveaxis((codes * scale).reshape(v.shape), -1, axis)


WIDE = False


def mx_kscale(k):
    if not WIDE:
        return np.ones(k)
    levels = np.array([10, -10, 5, -5, 0])
    if k % 512:
        return np.exp2(np.random.permutation(np.resize(levels, k // 32))).repeat(32)
    a = np.empty((k // 512, 16))
    for p in range(k // 512):
        a[p, :8] = np.random.permutation(np.resize(levels, 8))
        for g in range(8):
            far = levels[np.abs(levels - a[p, g]) >= 10]
            a[p, g + 8] = far[np.random.randint(len(far))]
    return np.exp2(a.ravel()).repeat(32)


def f64(x):
    return np.asarray(x).astype(np.float64)


def striped8(idx):
    return np.concatenate([v.reshape(-1, 16).T for v in idx]).astype(np.uint16)


def unstriped8(offs):
    return np.stack([offs[16 * g:16 * g + 16].T.reshape(-1) for g in range(8)]).astype(np.int64)


E2M1 = np.array([0.0, 0.5, 1.0, 1.5, 2.0, 3.0, 4.0, 6.0, -0.0, -0.5, -1.0, -1.5, -2.0, -3.0, -4.0, -6.0])


def pack_weight(w, fmt):
    k, n = w.shape
    w = f64(np.asarray(w, np.float32).astype(ml_dtypes.bfloat16)).reshape(k // 32, 32, n)
    amax = np.abs(w).max(1)
    if fmt == "e4m3":
        byte = np.frexp(amax)[1] - 1 + 127 - 7
    else:
        mant, ex = np.frexp(amax / 6.0)
        byte = np.where(mant > 0.5, ex, ex - 1) + 127
    byte = np.clip(np.where(amax > 0, byte, 1), 1, 254)
    scaled = (w * np.exp2(127.0 - byte)[:, None, :]).reshape(k, n).astype(np.float32)
    by_word = np.ascontiguousarray(scaled.reshape(k // 512, 128, 4, n).transpose(0, 1, 3, 2))
    if fmt == "e4m3":
        words = by_word.astype(ml_dtypes.float8_e4m3fn).view(np.uint8)
    else:
        c = by_word.astype(ml_dtypes.float4_e2m1fn).view(np.uint8) & 0xF
        words = (c[..., 0::2] | (c[..., 1::2] << 4)).reshape(k // 512, 128, 2 * n)
    return np.ascontiguousarray(words), np.ascontiguousarray(byte.astype(np.uint8).reshape(k // 512, 16, n))


def unpack_weight(words, scales, fmt):
    g, _, n = scales.shape
    words = np.ascontiguousarray(words).reshape(g, 128, n, -1)
    if fmt == "e4m3":
        vals = words.view(ml_dtypes.float8_e4m3fn).astype(np.float64)
    else:
        nib = np.empty((g, 128, n, 4), np.uint8)
        nib[..., 0::2] = words & 0xF
        nib[..., 1::2] = words >> 4
        vals = E2M1[nib]
    vals = vals * np.repeat(np.exp2(scales.astype(np.float64) - 127.0), 8, axis=1)[..., None]
    return vals.transpose(0, 1, 3, 2).reshape(g * 512, n)


def silu(v):
    return v / (1.0 + np.exp(-np.maximum(v, -700.0)))


K, M, T, S = 512, 256, 1024, 512


def setup_inputs():
    n = np.random.standard_normal
    s = mx_kscale(K)[:, None]
    u = mx_kscale(512)[:, None]
    p_w2 = pack_weight(1.4 * n((512, M)) / np.sqrt(512) / u, "e2m1")
    return {
        "xT": (n((K, T)) * s).astype(np.float32),
        "w1": (n((K, 512)) / np.sqrt(K) / s * u.T).astype(np.float32),
        "w2_words": p_w2[0],
        "w2_scales": p_w2[1],
        "wgt": np.repeat(np.random.uniform(0.5, 2.0, (8, S)), 16, axis=0).astype(np.float32),
        "b": (0.3 * n(256)).astype(np.float32),
        "wgo": np.repeat(np.random.uniform(0.5, 2.0, (8, S)), 16, axis=0).astype(np.float32),
        "offs": striped8(np.stack([np.random.permutation(T)[:S] for _ in range(8)])),
        "offs2": striped8(np.stack([np.random.permutation(T)[:S] for _ in range(8)])),
    }


def reference(xT, w1, w2_words, w2_scales, wgt, b, wgo, offs, offs2):
    idx = unstriped8(offs)
    group = np.arange(K) % 512 // 64
    xg = f64(wgt)[np.arange(K) // 4 % 128] * f64(xT)[np.arange(K)[:, None], idx[group]]
    xT_ = mxq(xg, 0, "e4m3")
    w1_ = mxq(f64(w1), 0, "e4m3")
    w2_ = unpack_weight(w2_words, w2_scales, "e2m1")
    h_ = mxq(np.maximum(w1_.T @ xT_, 0.0), 0, "e4m3")
    y = w2_.T @ h_
    place = unstriped8(offs2)[np.arange(M) % 128 // 16]
    out = np.zeros((M, T))
    out[np.arange(M)[:, None], place] = f64(wgo)[np.arange(M) % 128] * (silu(y + f64(b)[:, None]))
    return out

@@ -1,0 +1,189 @@
+from contextlib import ExitStack
+
+import concourse.mybir as mybir
+
+K, H, M, T, S = 512, 512, 256, 1024, 512
+FLOPS = 2 * K * H * S + 2 * H * M * S
+
+F32 = mybir.dt.float32
+BF16 = mybir.dt.bfloat16
+I32 = mybir.dt.int32
+U32 = mybir.dt.uint32
+U16 = mybir.dt.uint16
+U8 = mybir.dt.uint8
+FP8X4 = mybir.dt.float8_e4m3fn_x4
+FP4X4 = mybir.dt.float4_e2m1fn_x4
+MULT = mybir.AluOpType.mult
+ACT = mybir.ActivationFunctionType
+
+P = 128
+PACK = 4
+GROUP = 16
+HALF = S // 2
+CHUNK = 128
+W_HALF = H // 2
+M_HALF = W_HALF // PACK
+W1_VECTOR_M = (32, 40)
+
+
+def tile_list_hboth_m_silu_kernel(tc, xT, w1, w2_words, w2_scales, wgt, b, wgo, offs, offs2, out):
+    nc = tc.nc
+    with ExitStack() as ctx:
+        sb = ctx.enter_context(tc.tile_pool(name="sb", bufs=1))
+        ps = ctx.enter_context(tc.psum_pool(name="ps", bufs=1))
+
+        gather_list = sb.tile([P, S // GROUP], U16, name="gather_list")
+        scatter_list = sb.tile([P, S // GROUP], U16, name="scatter_list")
+        wgt_sb = sb.tile([P, S], F32, name="wgt_sb")
+        wgo_sb = sb.tile([P, S], F32, name="wgo_sb")
+        x_plane = [sb.tile([P, T], F32, name=f"x_plane{i}") for i in range(PACK)]
+        w1_raw = [sb.tile([P, PACK, W_HALF], F32, name=f"w1_raw{h}") for h in range(2)]
+        w1_bf = sb.tile([P, PACK, P, PACK], BF16, name="w1_bf", align_bytes=64)
+        w1_codes = sb.tile([P, PACK, P], U32, name="w1_codes", align_bytes=64)
+        w1_scales = sb.tile([P, PACK, P], U8, name="w1_scales", align_bytes=64)
+        w2_codes = sb.tile([P, 2 * M], U8, name="w2_codes", align_bytes=64)
+        w2_plane = sb.tile([P, M], U8, name="w2_plane", align_bytes=64)
+        bias = sb.tile([P, M // P], F32, name="bias")
+        window = [sb.tile([P, T], F32, name=f"window{blk}") for blk in range(M // P)]
+        picked = [sb.tile([P, PACK, HALF], F32, name=f"picked{a}") for a in range(2)]
+        xg_bf = [sb.tile([P, HALF, PACK], BF16, name=f"xg_bf{a}", align_bytes=64) for a in range(2)]
+        xg_codes = [sb.tile([P, HALF], U32, name=f"xg_codes{a}", align_bytes=64) for a in range(2)]
+        xg_scales = [sb.tile([P, HALF], U8, name=f"xg_scales{a}", align_bytes=64) for a in range(2)]
+        h_bf = [sb.tile([P, CHUNK, PACK], BF16, name=f"h_bf{c}", align_bytes=64) for c in range(4)]
+        h_codes = [sb.tile([P, CHUNK], U32, name=f"h_codes{c}", align_bytes=64) for c in range(4)]
+        h_scales = [sb.tile([P, CHUNK], U8, name=f"h_scales{c}", align_bytes=64) for c in range(4)]
+        y_sb = [[sb.tile([P, HALF], F32, name=f"y_sb{a}_{blk}") for blk in range(2)] for a in range(2)]
+        warm_in = sb.tile([P, 1], F32, name="warm_in")
+        warm_out = sb.tile([P, 1], F32, name="warm_out")
+        h_ps = [ps.tile([P, PACK, CHUNK], F32, name=f"h_ps{c}") for c in range(4)]
+        y_ps = [[ps.tile([P, HALF], F32, name=f"y_ps{a}_{blk}") for blk in range(2)] for a in range(2)]
+
+        nc.vector.memset(warm_in[:], 0.0)
+        nc.scalar.activation(warm_out[:], warm_in[:], ACT.Silu)
+        nc.vector.memset(w2_plane[:].bitcast(U32), 0)
+        for blk in range(2):
+            nc.vector.memset(window[blk][:], 0.0)
+
+        x_rows = xT.rearrange("(p i) t -> p i t", i=PACK)
+        w1_rows = w1.rearrange("(p j) c -> p j c", j=PACK)
+        nc.sync.dma_start(gather_list[:], offs)
+        nc.sync.dma_start(wgt_sb[:], wgt)
+        for i in range(PACK):
+            nc.sync.dma_start(x_plane[i][:], x_rows[:, i, :])
+        for h in range(2):
+            nc.sync.dma_start(w1_raw[h][:], w1_rows[:, :, h * W_HALF : (h + 1) * W_HALF])
+        nc.sync.dma_start(w2_codes[:].bitcast(I32), w2_words[0].bitcast(I32))
+        for q in range(4):
+            nc.sync.dma_start(w2_plane[32 * q : 32 * q + 4, :].bitcast(I32), w2_scales[0, 4 * q : 4 * q + 4, :].bitcast(I32))
+        with nc.allow_non_contiguous_dma(reason="one bias value a partition"):
+            nc.sync.dma_start(bias[:], b.rearrange("(c p) -> p c", p=P))
+        nc.sync.dma_start(scatter_list[:], offs2)
+        nc.sync.dma_start(wgo_sb[:], wgo)
+
+        def gather(a, i, lo, hi):
+            j0, j1 = a * HALF + lo, a * HALF + hi
+            nc.vector.tensor_tensor(
+                picked[a][:, i, lo:hi],
+                x_plane[i][:].indirect(gather_list[:, j0 // GROUP : j1 // GROUP]),
+                wgt_sb[:, j0:j1],
+                MULT,
+            )
+
+        def round_xg(copy, a, lo, hi):
+            copy(
+                xg_bf[a][:, lo:hi, :].rearrange("p (c n) i -> p c i n", n=4),
+                picked[a][:, :, lo:hi].rearrange("p i (c n) -> p c i n", n=4),
+            )
+
+        def quantize_xg(a):
+            nc.vector.quantize_mx(xg_codes[a][:].bitcast(FP8X4), xg_scales[a][:], xg_bf[a][:].rearrange("p n i -> p (n i)"))
+
+        def round_w1(copy, h, lo, hi):
+            copy(
+                w1_bf[:, :, h * M_HALF + lo : h * M_HALF + hi, :].rearrange("p t m j -> p m j t"),
+                w1_raw[h][:, :, PACK * lo : PACK * hi].rearrange("p j (m t) -> p m j t", t=PACK),
+            )
+
+        def round_w1_half(h):
+            round_w1(nc.vector.tensor_copy, h, 0, W1_VECTOR_M[h])
+            round_w1(nc.scalar.copy, h, W1_VECTOR_M[h], M_HALF)
+
+        def quantize_w1(h, t):
+            ms = slice(h * M_HALF, (h + 1) * M_HALF)
+            nc.vector.quantize_mx(
+                w1_codes[:, t, ms].bitcast(FP8X4), w1_scales[:, t, ms], w1_bf[:, t, ms, :].rearrange("p m j -> p (m j)")
+            )
+
+        def layer1(c):
+            a, cols = c // 2, slice(c % 2 * CHUNK, (c % 2 + 1) * CHUNK)
+            for t in range(PACK):
+                nc.tensor.matmul_mx(
+                    h_ps[c][:, t, :],
+                    lhsT=w1_codes[:, t, :].bitcast(FP8X4),
+                    lhsT_scale=w1_scales[:, t, :],
+                    rhs=xg_codes[a][:, cols].bitcast(FP8X4),
+                    rhs_scale=xg_scales[a][:, cols],
+                    start=True,
+                    stop=True,
+                )
+            nc.scalar.activation(h_bf[c][:], h_ps[c][:].rearrange("p t n -> p n t"), ACT.Relu)
+
+        def quantize_h(c):
+            nc.vector.quantize_mx(h_codes[c][:].bitcast(FP8X4), h_scales[c][:], h_bf[c][:].rearrange("p n t -> p (n t)"))
+
+        def layer2(a, blk):
+            for c in (2 * a, 2 * a + 1):
+                nc.tensor.matmul_mx(
+                    y_ps[a][blk][:, c % 2 * CHUNK : (c % 2 + 1) * CHUNK],
+                    lhsT=w2_codes[:, 2 * blk * P : 2 * (blk + 1) * P].bitcast(FP4X4),
+                    lhsT_scale=w2_plane[:, blk * P : (blk + 1) * P],
+                    rhs=h_codes[c][:].bitcast(FP8X4),
+                    rhs_scale=h_scales[c][:],
+                    start=True,
+                    stop=True,
+                )
+            nc.scalar.activation(y_sb[a][blk][:], y_ps[a][blk][:], ACT.Silu, bias=bias[:, blk : blk + 1])
+
+        def scatter(a, blk):
+            js = slice(a * HALF, (a + 1) * HALF)
+            nc.vector.tensor_tensor(
+                window[blk][:].indirect(scatter_list[:, js.start // GROUP : js.stop // GROUP]),
+                y_sb[a][blk][:],
+                wgo_sb[:, js],
+                MULT,
+            )
+
+        for i in range(PACK - 1):
+            for a in range(2):
+                gather(a, i, 0, HALF)
+        gather(0, PACK - 1, 0, CHUNK)
+        gather(0, PACK - 1, CHUNK, HALF)
+        round_xg(nc.vector.tensor_copy, 0, 0, CHUNK)
+        round_xg(nc.vector.tensor_copy, 0, CHUNK, HALF)
+        round_w1_half(0)
+        round_w1_half(1)
+        quantize_xg(0)
+        for h in range(2):
+            for t in range(PACK):
+                quantize_w1(h, t)
+        layer1(0)
+        layer1(1)
+        quantize_h(0)
+        quantize_h(1)
+        layer2(0, 0)
+        layer2(0, 1)
+
+        gather(1, PACK - 1, 0, HALF)
+        round_xg(nc.vector.tensor_copy, 1, 0, HALF)
+        quantize_xg(1)
+        layer1(2)
+        layer1(3)
+        scatter(0, 0)
+        quantize_h(2)
+        quantize_h(3)
+        layer2(1, 0)
+        layer2(1, 1)
+        scatter(0, 1)
+        for blk in range(2):
+            scatter(1, blk)
+            nc.sync.dma_start(out[blk * P : (blk + 1) * P, :], window[blk][:])

@@ -23,7 +23,6 @@ HALF = S // 2
 CHUNK = 128
 W_HALF = H // 2
 M_HALF = W_HALF // PACK
-W1_VECTOR_M = (32, 40)
 
 
 def tile_list_hboth_m_silu_kernel(tc, xT, w1, w2_words, w2_scales, wgt, b, wgo, offs, offs2, out):
@@ -32,52 +31,48 @@ def tile_list_hboth_m_silu_kernel(tc, xT, w1, w2_words, w2_scales, wgt, b, wgo, 
         sb = ctx.enter_context(tc.tile_pool(name="sb", bufs=1))
         ps = ctx.enter_context(tc.psum_pool(name="ps", bufs=1))
 
+        def mx_tile(shape, dtype, name, tag=None):
+            return sb.tile(shape, dtype, name=name, tag=tag or name, align_bytes=64)
+
         gather_list = sb.tile([P, S // GROUP], U16, name="gather_list")
         scatter_list = sb.tile([P, S // GROUP], U16, name="scatter_list")
-        wgt_sb = sb.tile([P, S], F32, name="wgt_sb")
+        wgt_sb = [sb.tile([P, HALF], F32, name=f"wgt_sb{a}") for a in range(2)]
         wgo_sb = sb.tile([P, S], F32, name="wgo_sb")
-        x_plane = [sb.tile([P, T], F32, name=f"x_plane{i}") for i in range(PACK)]
-        w1_raw = [sb.tile([P, PACK, W_HALF], F32, name=f"w1_raw{h}") for h in range(2)]
-        w1_bf = sb.tile([P, PACK, P, PACK], BF16, name="w1_bf", align_bytes=64)
-        w1_codes = sb.tile([P, PACK, P], U32, name="w1_codes", align_bytes=64)
-        w1_scales = sb.tile([P, PACK, P], U8, name="w1_scales", align_bytes=64)
-        w2_codes = sb.tile([P, 2 * M], U8, name="w2_codes", align_bytes=64)
-        w2_plane = sb.tile([P, M], U8, name="w2_plane", align_bytes=64)
+        x_plane = [mx_tile([P, T], F32, f"x_plane{i}") for i in range(PACK)]
+        w1_bf = [mx_tile([P, 2, P, PACK], BF16, f"w1_bf{u}") for u in range(2)]
+        w1_codes = mx_tile([P, PACK, P], U32, "w1_codes")
+        w1_scales = mx_tile([P, PACK, P], U8, "w1_scales")
+        w2_codes = mx_tile([P, 2 * M], U8, "w2_codes")
         bias = sb.tile([P, M // P], F32, name="bias")
         window = [sb.tile([P, T], F32, name=f"window{blk}") for blk in range(M // P)]
-        picked = [sb.tile([P, PACK, HALF], F32, name=f"picked{a}") for a in range(2)]
-        xg_bf = [sb.tile([P, HALF, PACK], BF16, name=f"xg_bf{a}", align_bytes=64) for a in range(2)]
-        xg_codes = [sb.tile([P, HALF], U32, name=f"xg_codes{a}", align_bytes=64) for a in range(2)]
-        xg_scales = [sb.tile([P, HALF], U8, name=f"xg_scales{a}", align_bytes=64) for a in range(2)]
-        h_bf = [sb.tile([P, CHUNK, PACK], BF16, name=f"h_bf{c}", align_bytes=64) for c in range(4)]
-        h_codes = [sb.tile([P, CHUNK], U32, name=f"h_codes{c}", align_bytes=64) for c in range(4)]
-        h_scales = [sb.tile([P, CHUNK], U8, name=f"h_scales{c}", align_bytes=64) for c in range(4)]
+        picked_first = sb.tile([P, PACK, HALF], F32, name="picked_first")
+        w1_first = sb.tile([P, PACK, W_HALF], F32, name="w1_first")
+        shared_rows = sb.tile([P, 2 * PACK - 1, HALF], F32, name="shared_rows")
+        picked = [picked_first[:], shared_rows[:, :PACK, :]]
+        w1_raw = [w1_first[:], shared_rows[:, PACK - 1 :, :]]
         y_sb = [[sb.tile([P, HALF], F32, name=f"y_sb{a}_{blk}") for blk in range(2)] for a in range(2)]
         warm_in = sb.tile([P, 1], F32, name="warm_in")
         warm_out = sb.tile([P, 1], F32, name="warm_out")
-        h_ps = [ps.tile([P, PACK, CHUNK], F32, name=f"h_ps{c}") for c in range(4)]
-        y_ps = [[ps.tile([P, HALF], F32, name=f"y_ps{a}_{blk}") for blk in range(2)] for a in range(2)]
 
         nc.vector.memset(warm_in[:], 0.0)
         nc.scalar.activation(warm_out[:], warm_in[:], ACT.Silu)
-        nc.vector.memset(w2_plane[:].bitcast(U32), 0)
         for blk in range(2):
             nc.vector.memset(window[blk][:], 0.0)
 
         x_rows = xT.rearrange("(p i) t -> p i t", i=PACK)
         w1_rows = w1.rearrange("(p j) c -> p j c", j=PACK)
         nc.sync.dma_start(gather_list[:], offs)
-        nc.sync.dma_start(wgt_sb[:], wgt)
-        for i in range(PACK):
+        nc.sync.dma_start(wgt_sb[0][:], wgt[:, :HALF])
+        nc.sync.dma_start(x_plane[0][:], x_rows[:, 0, :])
+        nc.sync.dma_start(wgt_sb[1][:], wgt[:, HALF:])
+        nc.sync.dma_start(scatter_list[:], offs2)
+        for i in range(1, PACK):
             nc.sync.dma_start(x_plane[i][:], x_rows[:, i, :])
         for h in range(2):
-            nc.sync.dma_start(w1_raw[h][:], w1_rows[:, :, h * W_HALF : (h + 1) * W_HALF])
+            nc.sync.dma_start(w1_raw[h], w1_rows[:, :, h * W_HALF : (h + 1) * W_HALF])
         nc.sync.dma_start(w2_codes[:].bitcast(I32), w2_words[0].bitcast(I32))
-        for q in range(4):
-            nc.sync.dma_start(w2_plane[32 * q : 32 * q + 4, :].bitcast(I32), w2_scales[0, 4 * q : 4 * q + 4, :].bitcast(I32))
         with nc.allow_non_contiguous_dma(reason="one bias value a partition"):
             nc.sync.dma_start(bias[:], b.rearrange("(c p) -> p c", p=P))
-        nc.sync.dma_start(scatter_list[:], offs2)
         nc.sync.dma_start(wgo_sb[:], wgo)
 
         def gather(a, i, lo, hi):
@@ -85,64 +80,58 @@ def tile_list_hboth_m_silu_kernel(tc, xT, w1, w2_words, w2_scales, wgt, b, wgo, 
             nc.vector.tensor_tensor(
                 picked[a][:, i, lo:hi],
                 x_plane[i][:].indirect(gather_list[:, j0 // GROUP : j1 // GROUP]),
-                wgt_sb[:, j0:j1],
+                wgt_sb[a][:, lo:hi],
                 MULT,
             )
 
-        def round_xg(copy, a, lo, hi):
+        def round_xg(copy, dst, a, lo, hi):
             copy(
-                xg_bf[a][:, lo:hi, :].rearrange("p (c n) i -> p c i n", n=4),
+                dst.rearrange("p (c n) i -> p c i n", n=4),
                 picked[a][:, :, lo:hi].rearrange("p i (c n) -> p c i n", n=4),
             )
 
-        def quantize_xg(a):
-            nc.vector.quantize_mx(xg_codes[a][:].bitcast(FP8X4), xg_scales[a][:], xg_bf[a][:].rearrange("p n i -> p (n i)"))
+        def quantize(src, width, name, tag=None, scales=None):
+            codes = mx_tile([P, width], U32, name + "_codes", tag)
+            if scales is None:
+                scales = mx_tile([P, width], U8, name + "_scales")[:]
+            nc.vector.quantize_mx(codes[:].bitcast(FP8X4), scales, src.rearrange("p n i -> p (n i)"))
+            return codes, scales
 
-        def round_w1(copy, h, lo, hi):
+        def round_w1(copy, h, u):
             copy(
-                w1_bf[:, :, h * M_HALF + lo : h * M_HALF + hi, :].rearrange("p t m j -> p m j t"),
-                w1_raw[h][:, :, PACK * lo : PACK * hi].rearrange("p j (m t) -> p m j t", t=PACK),
+                w1_bf[u][:, :, h * M_HALF : (h + 1) * M_HALF, :].rearrange("p t m j -> p m j t"),
+                w1_raw[h].rearrange("p j (m t) -> p m j t", t=PACK)[:, :, :, 2 * u : 2 * u + 2],
             )
 
-        def round_w1_half(h):
-            round_w1(nc.vector.tensor_copy, h, 0, W1_VECTOR_M[h])
-            round_w1(nc.scalar.copy, h, W1_VECTOR_M[h], M_HALF)
-
-        def quantize_w1(h, t):
-            ms = slice(h * M_HALF, (h + 1) * M_HALF)
-            nc.vector.quantize_mx(
-                w1_codes[:, t, ms].bitcast(FP8X4), w1_scales[:, t, ms], w1_bf[:, t, ms, :].rearrange("p m j -> p (m j)")
-            )
-
-        def layer1(c):
-            a, cols = c // 2, slice(c % 2 * CHUNK, (c % 2 + 1) * CHUNK)
+        def layer1(dst, operand, lo, name):
+            codes, scales = operand
+            h_ps = ps.tile([P, PACK, CHUNK], F32, name=name)
             for t in range(PACK):
                 nc.tensor.matmul_mx(
-                    h_ps[c][:, t, :],
+                    h_ps[:, t, :],
                     lhsT=w1_codes[:, t, :].bitcast(FP8X4),
                     lhsT_scale=w1_scales[:, t, :],
-                    rhs=xg_codes[a][:, cols].bitcast(FP8X4),
-                    rhs_scale=xg_scales[a][:, cols],
+                    rhs=codes[:, lo : lo + CHUNK].bitcast(FP8X4),
+                    rhs_scale=scales[:, lo : lo + CHUNK],
                     start=True,
                     stop=True,
                 )
-            nc.scalar.activation(h_bf[c][:], h_ps[c][:].rearrange("p t n -> p n t"), ACT.Relu)
+            nc.scalar.activation(dst, h_ps[:].rearrange("p t n -> p n t"), ACT.Relu)
 
-        def quantize_h(c):
-            nc.vector.quantize_mx(h_codes[c][:].bitcast(FP8X4), h_scales[c][:], h_bf[c][:].rearrange("p n t -> p (n t)"))
+        def layer2(dst, operand, blk):
+            codes, scales = operand
+            nc.tensor.matmul_mx(
+                dst,
+                lhsT=w2_codes[:, 2 * blk * P : 2 * (blk + 1) * P].bitcast(FP4X4),
+                lhsT_scale=w2_plane[:, blk * P : (blk + 1) * P],
+                rhs=codes[:].bitcast(FP8X4),
+                rhs_scale=scales,
+                start=True,
+                stop=True,
+            )
 
-        def layer2(a, blk):
-            for c in (2 * a, 2 * a + 1):
-                nc.tensor.matmul_mx(
-                    y_ps[a][blk][:, c % 2 * CHUNK : (c % 2 + 1) * CHUNK],
-                    lhsT=w2_codes[:, 2 * blk * P : 2 * (blk + 1) * P].bitcast(FP4X4),
-                    lhsT_scale=w2_plane[:, blk * P : (blk + 1) * P],
-                    rhs=h_codes[c][:].bitcast(FP8X4),
-                    rhs_scale=h_scales[c][:],
-                    start=True,
-                    stop=True,
-                )
-            nc.scalar.activation(y_sb[a][blk][:], y_ps[a][blk][:], ACT.Silu, bias=bias[:, blk : blk + 1])
+        def silu(a, blk, y_ps, lo, hi):
+            nc.scalar.activation(y_sb[a][blk][:, lo:hi], y_ps[:, lo:hi], ACT.Silu, bias=bias[:, blk : blk + 1])
 
         def scatter(a, blk):
             js = slice(a * HALF, (a + 1) * HALF)
@@ -156,34 +145,54 @@ def tile_list_hboth_m_silu_kernel(tc, xT, w1, w2_words, w2_scales, wgt, b, wgo, 
         for i in range(PACK - 1):
             for a in range(2):
                 gather(a, i, 0, HALF)
+        w2_plane = mx_tile([P, M], U8, "w2_plane", "x_plane0")
+        nc.vector.memset(w2_plane[:].bitcast(U32), 0)
+        for q in range(4):
+            nc.scalar.dma_start(w2_plane[32 * q : 32 * q + 4, :].bitcast(I32), w2_scales[0, 4 * q : 4 * q + 4, :].bitcast(I32))
         gather(0, PACK - 1, 0, CHUNK)
         gather(0, PACK - 1, CHUNK, HALF)
-        round_xg(nc.vector.tensor_copy, 0, 0, CHUNK)
-        round_xg(nc.vector.tensor_copy, 0, CHUNK, HALF)
-        round_w1_half(0)
-        round_w1_half(1)
-        quantize_xg(0)
+        xg_bf0 = mx_tile([P, CHUNK, PACK], BF16, "xg_bf0")
+        xg_bf1 = mx_tile([P, CHUNK, PACK], BF16, "xg_bf1")
+        round_xg(nc.scalar.copy, xg_bf0[:], 0, 0, CHUNK)
+        round_xg(nc.vector.tensor_copy, xg_bf1[:], 0, CHUNK, HALF)
+        xg0 = quantize(xg_bf0[:], CHUNK, "xg0")
+        xg1 = quantize(xg_bf1[:], CHUNK, "xg1", scales=w1_scales[4:, PACK - 1, :])
         for h in range(2):
-            for t in range(PACK):
-                quantize_w1(h, t)
-        layer1(0)
-        layer1(1)
-        quantize_h(0)
-        quantize_h(1)
-        layer2(0, 0)
-        layer2(0, 1)
+            round_w1(nc.vector.tensor_copy, h, 0)
+            round_w1(nc.scalar.copy, h, 1)
+        for t in range(PACK):
+            nc.vector.quantize_mx(w1_codes[:, t, :].bitcast(FP8X4), w1_scales[:, t, :], w1_bf[t // 2][:, t % 2, :, :].rearrange("p m j -> p (m j)"))
 
-        gather(1, PACK - 1, 0, HALF)
-        round_xg(nc.vector.tensor_copy, 1, 0, HALF)
-        quantize_xg(1)
-        layer1(2)
-        layer1(3)
+        h_bf = [mx_tile([P, CHUNK, PACK], BF16, f"h_bf{c}") for c in range(2)]
+        layer1(h_bf[0][:], xg0, 0, "h_ps0")
+        layer1(h_bf[1][:], xg1, 0, "h_ps1")
+        y_ps00 = ps.tile([P, HALF], F32, name="y_ps00")
+        h_first = []
+        for c in range(2):
+            h_first.append(quantize(h_bf[c][:], CHUNK, f"h{c}"))
+            layer2(y_ps00[:, c * CHUNK : (c + 1) * CHUNK], h_first[c], 0)
+            silu(0, 0, y_ps00, c * CHUNK, (c + 1) * CHUNK)
+
+        xg_bf2 = mx_tile([P, HALF, PACK], BF16, "xg_bf2")
+        for c in range(2):
+            gather(1, PACK - 1, c * CHUNK, (c + 1) * CHUNK)
+        for c in range(2):
+            round_xg(nc.vector.tensor_copy, xg_bf2[:, c * CHUNK : (c + 1) * CHUNK, :], 1, c * CHUNK, (c + 1) * CHUNK)
+        xg2 = quantize(xg_bf2[:], HALF, "xg2", "h_bf1")
         scatter(0, 0)
-        quantize_h(2)
-        quantize_h(3)
-        layer2(1, 0)
-        layer2(1, 1)
+        h_bf2 = mx_tile([P, HALF, PACK], BF16, "h_bf2")
+        for c in range(2):
+            layer1(h_bf2[:, c * CHUNK : (c + 1) * CHUNK, :], xg2, c * CHUNK, f"h_ps{2 + c}")
+        h_second = quantize(h_bf2[:], HALF, "h2")
+
+        y_ps01 = ps.tile([P, HALF], F32, name="y_ps01", tag="h_ps2")
+        for c in range(2):
+            layer2(y_ps01[:, c * CHUNK : (c + 1) * CHUNK], h_first[c], 1)
+        silu(0, 1, y_ps01, 0, HALF)
         scatter(0, 1)
         for blk in range(2):
+            y_ps1 = ps.tile([P, HALF], F32, name=f"y_ps1{blk}")
+            layer2(y_ps1[:], h_second, blk)
+            silu(1, blk, y_ps1, 0, HALF)
             scatter(1, blk)
             nc.sync.dma_start(out[blk * P : (blk + 1) * P, :], window[blk][:])

@@ -61,11 +61,10 @@ def tile_list_hboth_m_silu_kernel(tc, xT, w1, w2_words, w2_scales, wgt, b, wgo, 
 
         x_rows = xT.rearrange("(p i) t -> p i t", i=PACK)
         w1_rows = w1.rearrange("(p j) c -> p j c", j=PACK)
-        nc.sync.dma_start(gather_list[:], offs)
-        nc.sync.dma_start(wgt_sb[0][:], wgt[:, :HALF])
         nc.sync.dma_start(x_plane[0][:], x_rows[:, 0, :])
+        nc.sync.dma_start(wgt_sb[0][:], wgt[:, :HALF])
+        nc.sync.dma_start(gather_list[:], offs)
         nc.sync.dma_start(wgt_sb[1][:], wgt[:, HALF:])
-        nc.sync.dma_start(scatter_list[:], offs2)
         for i in range(1, PACK):
             nc.sync.dma_start(x_plane[i][:], x_rows[:, i, :])
         for h in range(2):
@@ -74,6 +73,7 @@ def tile_list_hboth_m_silu_kernel(tc, xT, w1, w2_words, w2_scales, wgt, b, wgo, 
         with nc.allow_non_contiguous_dma(reason="one bias value a partition"):
             nc.sync.dma_start(bias[:], b.rearrange("(c p) -> p c", p=P))
         nc.sync.dma_start(wgo_sb[:], wgo)
+        nc.sync.dma_start(scatter_list[:], offs2)
 
         def gather(a, i, lo, hi):
             j0, j1 = a * HALF + lo, a * HALF + hi
@@ -90,8 +90,8 @@ def tile_list_hboth_m_silu_kernel(tc, xT, w1, w2_words, w2_scales, wgt, b, wgo, 
                 picked[a][:, :, lo:hi].rearrange("p i (c n) -> p c i n", n=4),
             )
 
-        def quantize(src, width, name, tag=None, scales=None):
-            codes = mx_tile([P, width], U32, name + "_codes", tag)
+        def quantize(src, width, name, scales=None):
+            codes = mx_tile([P, width], U32, name + "_codes")
             if scales is None:
                 scales = mx_tile([P, width], U8, name + "_scales")[:]
             nc.vector.quantize_mx(codes[:].bitcast(FP8X4), scales, src.rearrange("p n i -> p (n i)"))
@@ -116,7 +116,7 @@ def tile_list_hboth_m_silu_kernel(tc, xT, w1, w2_words, w2_scales, wgt, b, wgo, 
                     start=True,
                     stop=True,
                 )
-            nc.scalar.activation(dst, h_ps[:].rearrange("p t n -> p n t"), ACT.Relu)
+            nc.scalar.activation(dst, h_ps[:].rearrange("p t n -> p n t"), ACT.Relu, bias=warm_out[:])
 
         def layer2(dst, operand, blk):
             codes, scales = operand
@@ -130,8 +130,8 @@ def tile_list_hboth_m_silu_kernel(tc, xT, w1, w2_words, w2_scales, wgt, b, wgo, 
                 stop=True,
             )
 
-        def silu(a, blk, y_ps, lo, hi):
-            nc.scalar.activation(y_sb[a][blk][:, lo:hi], y_ps[:, lo:hi], ACT.Silu, bias=bias[:, blk : blk + 1])
+        def silu(dst, y_ps, blk):
+            nc.scalar.activation(dst, y_ps, ACT.Silu, bias=bias[:, blk : blk + 1])
 
         def scatter(a, blk):
             js = slice(a * HALF, (a + 1) * HALF)
@@ -166,19 +166,23 @@ def tile_list_hboth_m_silu_kernel(tc, xT, w1, w2_words, w2_scales, wgt, b, wgo, 
         h_bf = [mx_tile([P, CHUNK, PACK], BF16, f"h_bf{c}") for c in range(2)]
         layer1(h_bf[0][:], xg0, 0, "h_ps0")
         layer1(h_bf[1][:], xg1, 0, "h_ps1")
-        y_ps00 = ps.tile([P, HALF], F32, name="y_ps00")
-        h_first = []
-        for c in range(2):
-            h_first.append(quantize(h_bf[c][:], CHUNK, f"h{c}"))
-            layer2(y_ps00[:, c * CHUNK : (c + 1) * CHUNK], h_first[c], 0)
-            silu(0, 0, y_ps00, c * CHUNK, (c + 1) * CHUNK)
 
+        def second_layer_first_block(c, scales=None):
+            operand = quantize(h_bf[c][:], CHUNK, f"h{c}", scales=scales)
+            y_ps = ps.tile([P, CHUNK], F32, name=f"y_ps_chunk{c}")
+            layer2(y_ps[:], operand, 0)
+            silu(y_sb[0][0][:, c * CHUNK : (c + 1) * CHUNK], y_ps[:], 0)
+            return operand
+
+        h_first = [second_layer_first_block(0)]
         xg_bf2 = mx_tile([P, HALF, PACK], BF16, "xg_bf2")
         for c in range(2):
             gather(1, PACK - 1, c * CHUNK, (c + 1) * CHUNK)
         for c in range(2):
             round_xg(nc.vector.tensor_copy, xg_bf2[:, c * CHUNK : (c + 1) * CHUNK, :], 1, c * CHUNK, (c + 1) * CHUNK)
-        xg2 = quantize(xg_bf2[:], HALF, "xg2", "h_bf1")
+        shared_scales = mx_tile([P, HALF], U8, "shared_scales")
+        xg2 = quantize(xg_bf2[:], HALF, "xg2", scales=shared_scales[4:, :])
+        h_first.append(second_layer_first_block(1, shared_scales[:, CHUNK // 2 : CHUNK // 2 + CHUNK]))
         scatter(0, 0)
         h_bf2 = mx_tile([P, HALF, PACK], BF16, "h_bf2")
         for c in range(2):
@@ -188,11 +192,11 @@ def tile_list_hboth_m_silu_kernel(tc, xT, w1, w2_words, w2_scales, wgt, b, wgo, 
         y_ps01 = ps.tile([P, HALF], F32, name="y_ps01", tag="h_ps2")
         for c in range(2):
             layer2(y_ps01[:, c * CHUNK : (c + 1) * CHUNK], h_first[c], 1)
-        silu(0, 1, y_ps01, 0, HALF)
+        silu(y_sb[0][1][:], y_ps01[:], 1)
         scatter(0, 1)
         for blk in range(2):
             y_ps1 = ps.tile([P, HALF], F32, name=f"y_ps1{blk}")
             layer2(y_ps1[:], h_second, blk)
-            silu(1, blk, y_ps1, 0, HALF)
+            silu(y_sb[1][blk][:], y_ps1[:], blk)
             scatter(1, blk)
             nc.sync.dma_start(out[blk * P : (blk + 1) * P, :], window[blk][:])

@@ -36,7 +36,7 @@ def tile_list_hboth_m_silu_kernel(tc, xT, w1, w2_words, w2_scales, wgt, b, wgo, 
 
         gather_list = sb.tile([P, S // GROUP], U16, name="gather_list")
         scatter_list = sb.tile([P, S // GROUP], U16, name="scatter_list")
-        wgt_sb = [sb.tile([P, HALF], F32, name=f"wgt_sb{a}") for a in range(2)]
+        wgt_sb = sb.tile([P, S], F32, name="wgt_sb")
         wgo_sb = sb.tile([P, S], F32, name="wgo_sb")
         x_plane = [mx_tile([P, T], F32, f"x_plane{i}") for i in range(PACK)]
         w1_bf = [mx_tile([P, 2, P, PACK], BF16, f"w1_bf{u}") for u in range(2)]
@@ -45,15 +45,20 @@ def tile_list_hboth_m_silu_kernel(tc, xT, w1, w2_words, w2_scales, wgt, b, wgo, 
         w2_codes = mx_tile([P, 2 * M], U8, "w2_codes")
         bias = sb.tile([P, M // P], F32, name="bias")
         window = [sb.tile([P, T], F32, name=f"window{blk}") for blk in range(M // P)]
-        picked_first = sb.tile([P, PACK, HALF], F32, name="picked_first")
         w1_first = sb.tile([P, PACK, W_HALF], F32, name="w1_first")
-        shared_rows = sb.tile([P, 2 * PACK - 1, HALF], F32, name="shared_rows")
-        picked = [picked_first[:], shared_rows[:, :PACK, :]]
-        w1_raw = [w1_first[:], shared_rows[:, PACK - 1 :, :]]
-        y_sb = [[sb.tile([P, HALF], F32, name=f"y_sb{a}_{blk}") for blk in range(2)] for a in range(2)]
+        shared = sb.tile([P, PACK * S - HALF + PACK * W_HALF], F32, name="shared")
+        picked = shared[:, : PACK * S].rearrange("p (i s) -> p i s", i=PACK)
+        w1_raw = [w1_first[:], shared[:, PACK * S - HALF :].rearrange("p (j c) -> p j c", j=PACK)]
+        y_sb = [sb.tile([P, S], F32, name=f"y_sb{blk}") for blk in range(2)]
+        xg_late = mx_tile([P, HALF, PACK], BF16, "xg_late")
+        xg_bf = [mx_tile([P, CHUNK, PACK], BF16, f"xg_bf{c}")[:] for c in range(2)]
         warm_in = sb.tile([P, 1], F32, name="warm_in")
         warm_out = sb.tile([P, 1], F32, name="warm_out")
 
+        w2_plane = mx_tile([P, M], U8, "w2_plane")
+        nc.gpsimd.memset(w2_plane[:].bitcast(U32), 0)
+        for q in range(4):
+            nc.gpsimd.dma_start(w2_plane[32 * q : 32 * q + 4, :].bitcast(I32), w2_scales[0, 4 * q : 4 * q + 4, :].bitcast(I32))
         nc.vector.memset(warm_in[:], 0.0)
         nc.scalar.activation(warm_out[:], warm_in[:], ACT.Silu)
         for blk in range(2):
@@ -62,9 +67,8 @@ def tile_list_hboth_m_silu_kernel(tc, xT, w1, w2_words, w2_scales, wgt, b, wgo, 
         x_rows = xT.rearrange("(p i) t -> p i t", i=PACK)
         w1_rows = w1.rearrange("(p j) c -> p j c", j=PACK)
         nc.sync.dma_start(x_plane[0][:], x_rows[:, 0, :])
-        nc.sync.dma_start(wgt_sb[0][:], wgt[:, :HALF])
         nc.sync.dma_start(gather_list[:], offs)
-        nc.sync.dma_start(wgt_sb[1][:], wgt[:, HALF:])
+        nc.sync.dma_start(wgt_sb[:], wgt)
         for i in range(1, PACK):
             nc.sync.dma_start(x_plane[i][:], x_rows[:, i, :])
         for h in range(2):
@@ -75,23 +79,26 @@ def tile_list_hboth_m_silu_kernel(tc, xT, w1, w2_words, w2_scales, wgt, b, wgo, 
         nc.sync.dma_start(wgo_sb[:], wgo)
         nc.sync.dma_start(scatter_list[:], offs2)
 
-        def gather(a, i, lo, hi):
-            j0, j1 = a * HALF + lo, a * HALF + hi
+        def gather(i, lo, hi):
             nc.vector.tensor_tensor(
-                picked[a][:, i, lo:hi],
-                x_plane[i][:].indirect(gather_list[:, j0 // GROUP : j1 // GROUP]),
-                wgt_sb[a][:, lo:hi],
+                picked[:, i, lo:hi],
+                x_plane[i][:].indirect(gather_list[:, lo // GROUP : hi // GROUP]),
+                wgt_sb[:, lo:hi],
                 MULT,
             )
 
-        def round_xg(copy, dst, a, lo, hi):
+        def round_xg(copy, dst, lo, hi, u):
             copy(
-                dst.rearrange("p (c n) i -> p c i n", n=4),
-                picked[a][:, :, lo:hi].rearrange("p i (c n) -> p c i n", n=4),
+                dst[:, :, 2 * u : 2 * u + 2].rearrange("p (c n) i -> p c i n", n=4),
+                picked[:, 2 * u : 2 * u + 2, lo:hi].rearrange("p i (c n) -> p c i n", n=4),
             )
 
-        def quantize(src, width, name, scales=None):
-            codes = mx_tile([P, width], U32, name + "_codes")
+        def quantize_w1(h, t):
+            ms = slice(h * M_HALF, (h + 1) * M_HALF)
+            nc.vector.quantize_mx(w1_codes[:, t, ms].bitcast(FP8X4), w1_scales[:, t, ms], w1_bf[t // 2][:, t % 2, ms, :].rearrange("p m j -> p (m j)"))
+
+        def quantize(src, width, name, tag=None, scales=None):
+            codes = mx_tile([P, width], U32, name + "_codes", tag)
             if scales is None:
                 scales = mx_tile([P, width], U8, name + "_scales")[:]
             nc.vector.quantize_mx(codes[:].bitcast(FP8X4), scales, src.rearrange("p n i -> p (n i)"))
@@ -103,12 +110,12 @@ def tile_list_hboth_m_silu_kernel(tc, xT, w1, w2_words, w2_scales, wgt, b, wgo, 
                 w1_raw[h].rearrange("p j (m t) -> p m j t", t=PACK)[:, :, :, 2 * u : 2 * u + 2],
             )
 
-        def layer1(dst, operand, lo, name):
+        def layer1(operand, name, lo=0, slices=range(PACK)):
             codes, scales = operand
-            h_ps = ps.tile([P, PACK, CHUNK], F32, name=name)
-            for t in range(PACK):
+            h_ps = ps.tile([P, len(slices), CHUNK], F32, name=name)
+            for k, t in enumerate(slices):
                 nc.tensor.matmul_mx(
-                    h_ps[:, t, :],
+                    h_ps[:, k, :],
                     lhsT=w1_codes[:, t, :].bitcast(FP8X4),
                     lhsT_scale=w1_scales[:, t, :],
                     rhs=codes[:, lo : lo + CHUNK].bitcast(FP8X4),
@@ -116,6 +123,9 @@ def tile_list_hboth_m_silu_kernel(tc, xT, w1, w2_words, w2_scales, wgt, b, wgo, 
                     start=True,
                     stop=True,
                 )
+            return h_ps
+
+        def relu(dst, h_ps):
             nc.scalar.activation(dst, h_ps[:].rearrange("p t n -> p n t"), ACT.Relu, bias=warm_out[:])
 
         def layer2(dst, operand, blk):
@@ -130,73 +140,69 @@ def tile_list_hboth_m_silu_kernel(tc, xT, w1, w2_words, w2_scales, wgt, b, wgo, 
                 stop=True,
             )
 
-        def silu(dst, y_ps, blk):
-            nc.scalar.activation(dst, y_ps, ACT.Silu, bias=bias[:, blk : blk + 1])
+        def silu(y_ps, blk, lo, hi):
+            nc.scalar.activation(y_sb[blk][:, lo:hi], y_ps, ACT.Silu, bias=bias[:, blk : blk + 1])
 
-        def scatter(a, blk):
-            js = slice(a * HALF, (a + 1) * HALF)
+        def scatter(blk, lo, hi):
             nc.vector.tensor_tensor(
-                window[blk][:].indirect(scatter_list[:, js.start // GROUP : js.stop // GROUP]),
-                y_sb[a][blk][:],
-                wgo_sb[:, js],
+                window[blk][:].indirect(scatter_list[:, lo // GROUP : hi // GROUP]),
+                y_sb[blk][:, lo:hi],
+                wgo_sb[:, lo:hi],
                 MULT,
             )
 
-        for i in range(PACK - 1):
-            for a in range(2):
-                gather(a, i, 0, HALF)
-        w2_plane = mx_tile([P, M], U8, "w2_plane", "x_plane0")
-        nc.vector.memset(w2_plane[:].bitcast(U32), 0)
-        for q in range(4):
-            nc.scalar.dma_start(w2_plane[32 * q : 32 * q + 4, :].bitcast(I32), w2_scales[0, 4 * q : 4 * q + 4, :].bitcast(I32))
-        gather(0, PACK - 1, 0, CHUNK)
-        gather(0, PACK - 1, CHUNK, HALF)
-        xg_bf0 = mx_tile([P, CHUNK, PACK], BF16, "xg_bf0")
-        xg_bf1 = mx_tile([P, CHUNK, PACK], BF16, "xg_bf1")
-        round_xg(nc.scalar.copy, xg_bf0[:], 0, 0, CHUNK)
-        round_xg(nc.vector.tensor_copy, xg_bf1[:], 0, CHUNK, HALF)
-        xg0 = quantize(xg_bf0[:], CHUNK, "xg0")
-        xg1 = quantize(xg_bf1[:], CHUNK, "xg1", scales=w1_scales[4:, PACK - 1, :])
-        for h in range(2):
-            round_w1(nc.vector.tensor_copy, h, 0)
-            round_w1(nc.scalar.copy, h, 1)
+        gather(0, 0, S)
+        gather(1, 0, S)
+        for c in range(2):
+            round_xg(nc.scalar.copy, xg_bf[c], c * CHUNK, (c + 1) * CHUNK, 0)
+        round_xg(nc.scalar.copy, xg_late[:], HALF, S, 0)
+        gather(2, 0, S)
+        for c in range(2):
+            gather(PACK - 1, c * CHUNK, (c + 1) * CHUNK)
+        for c in range(2):
+            round_xg(nc.vector.tensor_copy, xg_bf[c], c * CHUNK, (c + 1) * CHUNK, 1)
+        xg = [quantize(xg_bf[0], CHUNK, "xg0"), quantize(xg_bf[1], CHUNK, "xg1", scales=w1_scales[4:, PACK - 1, :])]
+        for u in range(2):
+            round_w1(nc.scalar.copy, 0, u)
+        for t in range(2):
+            quantize_w1(0, t)
+        round_w1(nc.vector.tensor_copy, 1, 0)
+        round_w1(nc.scalar.copy, 1, 1)
+        for t in range(2, PACK):
+            quantize_w1(0, t)
         for t in range(PACK):
-            nc.vector.quantize_mx(w1_codes[:, t, :].bitcast(FP8X4), w1_scales[:, t, :], w1_bf[t // 2][:, t % 2, :, :].rearrange("p m j -> p (m j)"))
+            quantize_w1(1, t)
 
         h_bf = [mx_tile([P, CHUNK, PACK], BF16, f"h_bf{c}") for c in range(2)]
-        layer1(h_bf[0][:], xg0, 0, "h_ps0")
-        layer1(h_bf[1][:], xg1, 0, "h_ps1")
+        for u in range(2):
+            relu(h_bf[0][:, :, 2 * u : 2 * u + 2], layer1(xg[0], f"h_ps0{u}", 0, range(2 * u, 2 * u + 2)))
+        relu(h_bf[1][:], layer1(xg[1], "h_ps1"))
+        gather(PACK - 1, HALF, S)
+        round_xg(nc.vector.tensor_copy, xg_late[:], HALF, S, 1)
 
-        def second_layer_first_block(c, scales=None):
-            operand = quantize(h_bf[c][:], CHUNK, f"h{c}", scales=scales)
-            y_ps = ps.tile([P, CHUNK], F32, name=f"y_ps_chunk{c}")
-            layer2(y_ps[:], operand, 0)
-            silu(y_sb[0][0][:, c * CHUNK : (c + 1) * CHUNK], y_ps[:], 0)
-            return operand
-
-        h_first = [second_layer_first_block(0)]
-        xg_bf2 = mx_tile([P, HALF, PACK], BF16, "xg_bf2")
-        for c in range(2):
-            gather(1, PACK - 1, c * CHUNK, (c + 1) * CHUNK)
-        for c in range(2):
-            round_xg(nc.vector.tensor_copy, xg_bf2[:, c * CHUNK : (c + 1) * CHUNK, :], 1, c * CHUNK, (c + 1) * CHUNK)
-        shared_scales = mx_tile([P, HALF], U8, "shared_scales")
-        xg2 = quantize(xg_bf2[:], HALF, "xg2", scales=shared_scales[4:, :])
-        h_first.append(second_layer_first_block(1, shared_scales[:, CHUNK // 2 : CHUNK // 2 + CHUNK]))
-        scatter(0, 0)
-        h_bf2 = mx_tile([P, HALF, PACK], BF16, "h_bf2")
-        for c in range(2):
-            layer1(h_bf2[:, c * CHUNK : (c + 1) * CHUNK, :], xg2, c * CHUNK, f"h_ps{2 + c}")
-        h_second = quantize(h_bf2[:], HALF, "h2")
-
-        y_ps01 = ps.tile([P, HALF], F32, name="y_ps01", tag="h_ps2")
-        for c in range(2):
-            layer2(y_ps01[:, c * CHUNK : (c + 1) * CHUNK], h_first[c], 1)
-        silu(y_sb[0][1][:], y_ps01[:], 1)
-        scatter(0, 1)
+        h0 = quantize(h_bf[0][:], CHUNK, "h0")
         for blk in range(2):
-            y_ps1 = ps.tile([P, HALF], F32, name=f"y_ps1{blk}")
-            layer2(y_ps1[:], h_second, blk)
-            silu(y_sb[1][blk][:], y_ps1[:], blk)
-            scatter(1, blk)
+            y_ps = ps.tile([P, CHUNK], F32, name=f"y_ps0{blk}")
+            layer2(y_ps[:], h0, blk)
+            silu(y_ps[:], blk, 0, CHUNK)
+        xg2 = quantize(xg_late[:], HALF, "xg2", tag="h_bf0")
+        h1 = quantize(h_bf[1][:], CHUNK, "h1")
+        for blk in range(2):
+            scatter(blk, 0, CHUNK)
+        h_bf2 = mx_tile([P, HALF, PACK], BF16, "h_bf2", "h0_codes")
+        for c in range(2):
+            relu(h_bf2[:, c * CHUNK : (c + 1) * CHUNK, :], layer1(xg2, f"h_ps{2 + c}", c * CHUNK))
+        y_ps1 = ps.tile([P, 2, CHUNK], F32, name="y_ps1")
+        for blk in range(2):
+            layer2(y_ps1[:, blk, :], h1, blk)
+        for blk in range(2):
+            silu(y_ps1[:, blk, :], blk, CHUNK, HALF)
+        h2 = quantize(h_bf2[:], HALF, "h2")
+        for blk in range(2):
+            scatter(blk, CHUNK, HALF)
+        for blk in range(2):
+            y_ps2 = ps.tile([P, HALF], F32, name=f"y_ps2{blk}", tag=f"h_ps0{blk}")
+            layer2(y_ps2[:], h2, blk)
+            silu(y_ps2[:], blk, HALF, S)
+            scatter(blk, HALF, S)
             nc.sync.dma_start(out[blk * P : (blk + 1) * P, :], window[blk][:])

@@ -23,6 +23,7 @@ HALF = S // 2
 CHUNK = 128
 W_HALF = H // 2
 M_HALF = W_HALF // PACK
+BLOCK = 32
 
 
 def tile_list_hboth_m_silu_kernel(tc, xT, w1, w2_words, w2_scales, wgt, b, wgo, offs, offs2, out):
@@ -36,7 +37,10 @@ def tile_list_hboth_m_silu_kernel(tc, xT, w1, w2_words, w2_scales, wgt, b, wgo, 
 
         gather_list = sb.tile([P, S // GROUP], U16, name="gather_list")
         scatter_list = sb.tile([P, S // GROUP], U16, name="scatter_list")
-        wgt_sb = sb.tile([P, S], F32, name="wgt_sb")
+        wgt_rows = mx_tile([P, BLOCK], F32, "wgt_rows")
+        wgt_turned = mx_tile([P, BLOCK], F32, "wgt_turned")
+        wgt_spread = mx_tile([P, S], F32, "wgt_spread")
+        wgt_sb = mx_tile([P, S], F32, "wgt_sb")
         wgo_sb = sb.tile([P, S], F32, name="wgo_sb")
         x_plane = [mx_tile([P, T], F32, f"x_plane{i}") for i in range(PACK)]
         w1_bf = [mx_tile([P, 2, P, PACK], BF16, f"w1_bf{u}") for u in range(2)]
@@ -61,14 +65,14 @@ def tile_list_hboth_m_silu_kernel(tc, xT, w1, w2_words, w2_scales, wgt, b, wgo, 
             nc.gpsimd.dma_start(w2_plane[32 * q : 32 * q + 4, :].bitcast(I32), w2_scales[0, 4 * q : 4 * q + 4, :].bitcast(I32))
         nc.vector.memset(warm_in[:], 0.0)
         nc.scalar.activation(warm_out[:], warm_in[:], ACT.Silu)
-        for blk in range(2):
-            nc.vector.memset(window[blk][:], 0.0)
+        nc.vector.memset(window[0][:], 0.0)
+        nc.gpsimd.memset(window[1][:], 0.0)
 
         x_rows = xT.rearrange("(p i) t -> p i t", i=PACK)
         w1_rows = w1.rearrange("(p j) c -> p j c", j=PACK)
+        nc.sync.dma_start(wgt_rows[:], wgt.rearrange("(g r) (n c) -> g r n c", r=GROUP, c=BLOCK)[:, 0, :, :])
         nc.sync.dma_start(x_plane[0][:], x_rows[:, 0, :])
         nc.sync.dma_start(gather_list[:], offs)
-        nc.sync.dma_start(wgt_sb[:], wgt)
         for i in range(1, PACK):
             nc.sync.dma_start(x_plane[i][:], x_rows[:, i, :])
         for h in range(2):
@@ -151,6 +155,15 @@ def tile_list_hboth_m_silu_kernel(tc, xT, w1, w2_words, w2_scales, wgt, b, wgo, 
                 MULT,
             )
 
+        nc.vector.transpose(wgt_turned[:], wgt_rows[:])
+        blocks = HALF // BLOCK
+        for a in range(2):
+            nc.vector.tensor_copy(
+                wgt_spread[:, a * HALF : (a + 1) * HALF].rearrange("p (n g r) -> p n g r", g=2, r=GROUP),
+                wgt_turned[:].rearrange("p (g n) -> p n g", g=2)[:, a * blocks : (a + 1) * blocks, :].unsqueeze(3).to_broadcast([P, blocks, 2, GROUP]),
+            )
+        for a in range(2):
+            nc.vector.transpose(wgt_sb[:, a * HALF : (a + 1) * HALF], wgt_spread[:, a * HALF : (a + 1) * HALF])
         gather(0, 0, S)
         gather(1, 0, S)
         for c in range(2):

@@ -48,12 +48,12 @@ def tile_list_hboth_m_silu_kernel(tc, xT, w1, w2_words, w2_scales, wgt, b, wgo, 
         w1_scales = mx_tile([P, PACK, P], U8, "w1_scales")
         w2_codes = mx_tile([P, 2 * M], U8, "w2_codes")
         bias = sb.tile([P, M // P], F32, name="bias")
-        window = [sb.tile([P, T], F32, name=f"window{blk}") for blk in range(M // P)]
+        window = [sb.tile([P, T], F32, name="window0")]
         w1_first = sb.tile([P, PACK, W_HALF], F32, name="w1_first")
         shared = sb.tile([P, PACK * S - HALF + PACK * W_HALF], F32, name="shared")
         picked = shared[:, : PACK * S].rearrange("p (i s) -> p i s", i=PACK)
         w1_raw = [w1_first[:], shared[:, PACK * S - HALF :].rearrange("p (j c) -> p j c", j=PACK)]
-        y_sb = [sb.tile([P, S], F32, name=f"y_sb{blk}") for blk in range(2)]
+        y_sb = {(blk, lo): mx_tile([P, hi - lo], F32, f"y_sb{blk}_{lo}") for blk in range(2) for lo, hi in ((0, CHUNK), (CHUNK, HALF), (HALF, S))}
         xg_late = mx_tile([P, HALF, PACK], BF16, "xg_late")
         xg_bf = [mx_tile([P, CHUNK, PACK], BF16, f"xg_bf{c}")[:] for c in range(2)]
         warm_in = sb.tile([P, 1], F32, name="warm_in")
@@ -61,12 +61,15 @@ def tile_list_hboth_m_silu_kernel(tc, xT, w1, w2_words, w2_scales, wgt, b, wgo, 
 
         w2_plane = mx_tile([P, M], U8, "w2_plane")
         nc.gpsimd.memset(w2_plane[:].bitcast(U32), 0)
-        for q in range(4):
-            nc.gpsimd.dma_start(w2_plane[32 * q : 32 * q + 4, :].bitcast(I32), w2_scales[0, 4 * q : 4 * q + 4, :].bitcast(I32))
+
+        def load_scale_rows(queue, q):
+            queue.dma_start(w2_plane[32 * q : 32 * q + 4, :].bitcast(I32), w2_scales[0, 4 * q : 4 * q + 4, :].bitcast(I32))
+
+        for q in range(2):
+            load_scale_rows(nc.gpsimd, q)
         nc.vector.memset(warm_in[:], 0.0)
         nc.scalar.activation(warm_out[:], warm_in[:], ACT.Silu)
         nc.vector.memset(window[0][:], 0.0)
-        nc.gpsimd.memset(window[1][:], 0.0)
 
         x_rows = xT.rearrange("(p i) t -> p i t", i=PACK)
         w1_rows = w1.rearrange("(p j) c -> p j c", j=PACK)
@@ -77,6 +80,8 @@ def tile_list_hboth_m_silu_kernel(tc, xT, w1, w2_words, w2_scales, wgt, b, wgo, 
             nc.sync.dma_start(x_plane[i][:], x_rows[:, i, :])
         for h in range(2):
             nc.sync.dma_start(w1_raw[h], w1_rows[:, :, h * W_HALF : (h + 1) * W_HALF])
+        for q in range(2, 4):
+            load_scale_rows(nc.sync, q)
         nc.sync.dma_start(w2_codes[:].bitcast(I32), w2_words[0].bitcast(I32))
         with nc.allow_non_contiguous_dma(reason="one bias value a partition"):
             nc.sync.dma_start(bias[:], b.rearrange("(c p) -> p c", p=P))
@@ -145,12 +150,12 @@ def tile_list_hboth_m_silu_kernel(tc, xT, w1, w2_words, w2_scales, wgt, b, wgo, 
             )
 
         def silu(y_ps, blk, lo, hi):
-            nc.scalar.activation(y_sb[blk][:, lo:hi], y_ps, ACT.Silu, bias=bias[:, blk : blk + 1])
+            nc.scalar.activation(y_sb[blk, lo][:], y_ps, ACT.Silu, bias=bias[:, blk : blk + 1])
 
         def scatter(blk, lo, hi):
             nc.vector.tensor_tensor(
                 window[blk][:].indirect(scatter_list[:, lo // GROUP : hi // GROUP]),
-                y_sb[blk][:, lo:hi],
+                y_sb[blk, lo][:],
                 wgo_sb[:, lo:hi],
                 MULT,
             )
@@ -158,13 +163,16 @@ def tile_list_hboth_m_silu_kernel(tc, xT, w1, w2_words, w2_scales, wgt, b, wgo, 
         nc.vector.transpose(wgt_turned[:], wgt_rows[:])
         blocks = HALF // BLOCK
         for a in range(2):
-            nc.vector.tensor_copy(
+            nc.scalar.copy(
                 wgt_spread[:, a * HALF : (a + 1) * HALF].rearrange("p (n g r) -> p n g r", g=2, r=GROUP),
                 wgt_turned[:].rearrange("p (g n) -> p n g", g=2)[:, a * blocks : (a + 1) * blocks, :].unsqueeze(3).to_broadcast([P, blocks, 2, GROUP]),
             )
         for a in range(2):
             nc.vector.transpose(wgt_sb[:, a * HALF : (a + 1) * HALF], wgt_spread[:, a * HALF : (a + 1) * HALF])
-        gather(0, 0, S)
+        window.append(mx_tile([P, T], F32, "window1", "wgt_turned"))
+        nc.gpsimd.memset(window[1][:], 0.0)
+        for a in range(2):
+            gather(0, a * HALF, (a + 1) * HALF)
         gather(1, 0, S)
         for c in range(2):
             round_xg(nc.scalar.copy, xg_bf[c], c * CHUNK, (c + 1) * CHUNK, 0)
@@ -210,7 +218,10 @@ def tile_list_hboth_m_silu_kernel(tc, xT, w1, w2_words, w2_scales, wgt, b, wgo, 
             layer2(y_ps1[:, blk, :], h1, blk)
         for blk in range(2):
             silu(y_ps1[:, blk, :], blk, CHUNK, HALF)
-        h2 = quantize(h_bf2[:], HALF, "h2")
+        h2 = mx_tile([P, HALF], U32, "h2_codes", "y_sb0_0"), mx_tile([P, HALF], U8, "h2_scales")[:]
+        for c in range(2):
+            cols = slice(c * CHUNK, (c + 1) * CHUNK)
+            nc.vector.quantize_mx(h2[0][:, cols].bitcast(FP8X4), h2[1][:, cols], h_bf2[:, cols, :].rearrange("p n i -> p (n i)"))
         for blk in range(2):
             scatter(blk, CHUNK, HALF)
         for blk in range(2):

@@ -50,23 +50,16 @@ def tile_list_hboth_m_silu_kernel(tc, xT, w1, w2_words, w2_scales, wgt, b, wgo, 
         bias = sb.tile([P, M // P], F32, name="bias")
         window = [sb.tile([P, T], F32, name="window0")]
         w1_first = sb.tile([P, PACK, W_HALF], F32, name="w1_first")
-        shared = sb.tile([P, PACK * S - HALF + PACK * W_HALF], F32, name="shared")
+        raw_end = PACK * S - HALF + PACK * W_HALF
+        shared = mx_tile([P, raw_end + HALF], F32, "shared")
         picked = shared[:, : PACK * S].rearrange("p (i s) -> p i s", i=PACK)
-        w1_raw = [w1_first[:], shared[:, PACK * S - HALF :].rearrange("p (j c) -> p j c", j=PACK)]
+        w1_raw = [w1_first[:], shared[:, PACK * S - HALF : raw_end].rearrange("p (j c) -> p j c", j=PACK)]
         y_sb = {(blk, lo): mx_tile([P, hi - lo], F32, f"y_sb{blk}_{lo}") for blk in range(2) for lo, hi in ((0, CHUNK), (CHUNK, HALF), (HALF, S))}
-        xg_late = mx_tile([P, HALF, PACK], BF16, "xg_late")
+        xg_late = shared[:, raw_end - HALF :].bitcast(BF16).rearrange("p (n i) -> p n i", i=PACK)
         xg_bf = [mx_tile([P, CHUNK, PACK], BF16, f"xg_bf{c}")[:] for c in range(2)]
         warm_in = sb.tile([P, 1], F32, name="warm_in")
         warm_out = sb.tile([P, 1], F32, name="warm_out")
 
-        w2_plane = mx_tile([P, M], U8, "w2_plane")
-        nc.gpsimd.memset(w2_plane[:].bitcast(U32), 0)
-
-        def load_scale_rows(queue, q):
-            queue.dma_start(w2_plane[32 * q : 32 * q + 4, :].bitcast(I32), w2_scales[0, 4 * q : 4 * q + 4, :].bitcast(I32))
-
-        for q in range(2):
-            load_scale_rows(nc.gpsimd, q)
         nc.vector.memset(warm_in[:], 0.0)
         nc.scalar.activation(warm_out[:], warm_in[:], ACT.Silu)
         nc.vector.memset(window[0][:], 0.0)
@@ -80,13 +73,6 @@ def tile_list_hboth_m_silu_kernel(tc, xT, w1, w2_words, w2_scales, wgt, b, wgo, 
             nc.sync.dma_start(x_plane[i][:], x_rows[:, i, :])
         for h in range(2):
             nc.sync.dma_start(w1_raw[h], w1_rows[:, :, h * W_HALF : (h + 1) * W_HALF])
-        for q in range(2, 4):
-            load_scale_rows(nc.sync, q)
-        nc.sync.dma_start(w2_codes[:].bitcast(I32), w2_words[0].bitcast(I32))
-        with nc.allow_non_contiguous_dma(reason="one bias value a partition"):
-            nc.sync.dma_start(bias[:], b.rearrange("(c p) -> p c", p=P))
-        nc.sync.dma_start(wgo_sb[:], wgo)
-        nc.sync.dma_start(scatter_list[:], offs2)
 
         def gather(i, lo, hi):
             nc.vector.tensor_tensor(
@@ -163,32 +149,49 @@ def tile_list_hboth_m_silu_kernel(tc, xT, w1, w2_words, w2_scales, wgt, b, wgo, 
         nc.vector.transpose(wgt_turned[:], wgt_rows[:])
         blocks = HALF // BLOCK
         for a in range(2):
-            nc.scalar.copy(
+            nc.vector.tensor_copy(
                 wgt_spread[:, a * HALF : (a + 1) * HALF].rearrange("p (n g r) -> p n g r", g=2, r=GROUP),
                 wgt_turned[:].rearrange("p (g n) -> p n g", g=2)[:, a * blocks : (a + 1) * blocks, :].unsqueeze(3).to_broadcast([P, blocks, 2, GROUP]),
             )
         for a in range(2):
             nc.vector.transpose(wgt_sb[:, a * HALF : (a + 1) * HALF], wgt_spread[:, a * HALF : (a + 1) * HALF])
-        window.append(mx_tile([P, T], F32, "window1", "wgt_turned"))
+        w2_plane = mx_tile([P, M], U8, "w2_plane", "wgt_turned")
+        nc.gpsimd.memset(w2_plane[:].bitcast(U32), 0)
+
+        def load_scale_rows(queue, q):
+            queue.dma_start(w2_plane[32 * q : 32 * q + 4, :].bitcast(I32), w2_scales[0, 4 * q : 4 * q + 4, :].bitcast(I32))
+
+        for q in range(2):
+            load_scale_rows(nc.gpsimd, q)
+        for q in range(2, 4):
+            load_scale_rows(nc.sync, q)
+        nc.sync.dma_start(w2_codes[:].bitcast(I32), w2_words[0].bitcast(I32))
+        with nc.allow_non_contiguous_dma(reason="one bias value a partition"):
+            nc.sync.dma_start(bias[:], b.rearrange("(c p) -> p c", p=P))
+        nc.sync.dma_start(wgo_sb[:], wgo)
+        nc.sync.dma_start(scatter_list[:], offs2)
+
+        window.append(mx_tile([P, T], F32, "window1", "wgt_spread"))
         nc.gpsimd.memset(window[1][:], 0.0)
         for a in range(2):
             gather(0, a * HALF, (a + 1) * HALF)
         gather(1, 0, S)
         for c in range(2):
             round_xg(nc.scalar.copy, xg_bf[c], c * CHUNK, (c + 1) * CHUNK, 0)
-        round_xg(nc.scalar.copy, xg_late[:], HALF, S, 0)
+        round_xg(nc.scalar.copy, xg_late[:, CHUNK:, :], S - CHUNK, S, 0)
         gather(2, 0, S)
         for c in range(2):
             gather(PACK - 1, c * CHUNK, (c + 1) * CHUNK)
         for c in range(2):
             round_xg(nc.vector.tensor_copy, xg_bf[c], c * CHUNK, (c + 1) * CHUNK, 1)
-        xg = [quantize(xg_bf[0], CHUNK, "xg0"), quantize(xg_bf[1], CHUNK, "xg1", scales=w1_scales[4:, PACK - 1, :])]
+        xg0 = quantize(xg_bf[0], CHUNK, "xg0")
         for u in range(2):
             round_w1(nc.scalar.copy, 0, u)
         for t in range(2):
             quantize_w1(0, t)
         round_w1(nc.vector.tensor_copy, 1, 0)
         round_w1(nc.scalar.copy, 1, 1)
+        round_xg(nc.scalar.copy, xg_late[:, :CHUNK, :], HALF, HALF + CHUNK, 0)
         for t in range(2, PACK):
             quantize_w1(0, t)
         for t in range(PACK):
@@ -196,17 +199,18 @@ def tile_list_hboth_m_silu_kernel(tc, xT, w1, w2_words, w2_scales, wgt, b, wgo, 
 
         h_bf = [mx_tile([P, CHUNK, PACK], BF16, f"h_bf{c}") for c in range(2)]
         for u in range(2):
-            relu(h_bf[0][:, :, 2 * u : 2 * u + 2], layer1(xg[0], f"h_ps0{u}", 0, range(2 * u, 2 * u + 2)))
-        relu(h_bf[1][:], layer1(xg[1], "h_ps1"))
+            relu(h_bf[0][:, :, 2 * u : 2 * u + 2], layer1(xg0, f"h_ps0{u}", 0, range(2 * u, 2 * u + 2)))
         gather(PACK - 1, HALF, S)
-        round_xg(nc.vector.tensor_copy, xg_late[:], HALF, S, 1)
+        xg1 = quantize(xg_bf[1], CHUNK, "xg1", scales=w1_scales[4:, PACK - 1, :])
+        relu(h_bf[1][:], layer1(xg1, "h_ps1"))
+        round_xg(nc.vector.tensor_copy, xg_late, HALF, S, 1)
 
         h0 = quantize(h_bf[0][:], CHUNK, "h0")
         for blk in range(2):
             y_ps = ps.tile([P, CHUNK], F32, name=f"y_ps0{blk}")
             layer2(y_ps[:], h0, blk)
             silu(y_ps[:], blk, 0, CHUNK)
-        xg2 = quantize(xg_late[:], HALF, "xg2", tag="h_bf0")
+        xg2 = quantize(xg_late, HALF, "xg2", tag="h_bf0")
         h1 = quantize(h_bf[1][:], CHUNK, "h1")
         for blk in range(2):
             scatter(blk, 0, CHUNK)

@@ -66,7 +66,7 @@ def tile_list_hboth_m_silu_kernel(tc, xT, w1, w2_words, w2_scales, wgt, b, wgo, 
 
         x_rows = xT.rearrange("(p i) t -> p i t", i=PACK)
         w1_rows = w1.rearrange("(p j) c -> p j c", j=PACK)
-        nc.sync.dma_start(wgt_rows[:], wgt.rearrange("(g r) (n c) -> g r n c", r=GROUP, c=BLOCK)[:, 0, :, :])
+        nc.sync.dma_start(wgt_rows[:], wgt.rearrange("p (a c) -> (p a) c", c=HALF)[:: GROUP + 1, :].rearrange("u (n c) -> u n c", c=BLOCK))
         nc.sync.dma_start(x_plane[0][:], x_rows[:, 0, :])
         nc.sync.dma_start(gather_list[:], offs)
         for i in range(1, PACK):

@@ -23,6 +23,7 @@ HALF = S // 2
 CHUNK = 128
 W_HALF = H // 2
 M_HALF = W_HALF // PACK
+M_QUARTER = M_HALF // 2
 BLOCK = 32
 
 
@@ -43,7 +44,8 @@ def tile_list_hboth_m_silu_kernel(tc, xT, w1, w2_words, w2_scales, wgt, b, wgo, 
         wgt_sb = mx_tile([P, S], F32, "wgt_sb")
         wgo_sb = sb.tile([P, S], F32, name="wgo_sb")
         x_plane = [mx_tile([P, T], F32, f"x_plane{i}") for i in range(PACK)]
-        w1_bf = [mx_tile([P, 2, P, PACK], BF16, f"w1_bf{u}") for u in range(2)]
+        w1_bf = [mx_tile([P, 2, M_HALF, PACK], BF16, f"w1_bf{u}") for u in range(2)]
+        w1_last_bf = {(u, q): mx_tile([P, 2, M_QUARTER, PACK], BF16, f"w1_last_bf{u}{q}") for u in range(2) for q in range(2)}
         w1_codes = mx_tile([P, PACK, P], U32, "w1_codes")
         w1_scales = mx_tile([P, PACK, P], U8, "w1_scales")
         w2_codes = mx_tile([P, 2 * M], U8, "w2_codes")
@@ -60,6 +62,8 @@ def tile_list_hboth_m_silu_kernel(tc, xT, w1, w2_words, w2_scales, wgt, b, wgo, 
         warm_in = sb.tile([P, 1], F32, name="warm_in")
         warm_out = sb.tile([P, 1], F32, name="warm_out")
 
+        w2_plane = mx_tile([P, M], U8, "w2_plane")
+        nc.vector.memset(w2_plane[:].bitcast(U32), 0)
         nc.vector.memset(warm_in[:], 0.0)
         nc.scalar.activation(warm_out[:], warm_in[:], ACT.Silu)
         nc.vector.memset(window[0][:], 0.0)
@@ -92,10 +96,9 @@ def tile_list_hboth_m_silu_kernel(tc, xT, w1, w2_words, w2_scales, wgt, b, wgo, 
             ms = slice(h * M_HALF, (h + 1) * M_HALF)
             nc.vector.quantize_mx(w1_codes[:, t, ms].bitcast(FP8X4), w1_scales[:, t, ms], w1_bf[t // 2][:, t % 2, ms, :].rearrange("p m j -> p (m j)"))
 
-        def quantize(src, width, name, tag=None, scales=None):
+        def quantize(src, width, name, tag=None):
             codes = mx_tile([P, width], U32, name + "_codes", tag)
-            if scales is None:
-                scales = mx_tile([P, width], U8, name + "_scales")[:]
+            scales = mx_tile([P, width], U8, name + "_scales")[:]
             nc.vector.quantize_mx(codes[:].bitcast(FP8X4), scales, src.rearrange("p n i -> p (n i)"))
             return codes, scales
 
@@ -155,8 +158,6 @@ def tile_list_hboth_m_silu_kernel(tc, xT, w1, w2_words, w2_scales, wgt, b, wgo, 
             )
         for a in range(2):
             nc.vector.transpose(wgt_sb[:, a * HALF : (a + 1) * HALF], wgt_spread[:, a * HALF : (a + 1) * HALF])
-        w2_plane = mx_tile([P, M], U8, "w2_plane", "wgt_turned")
-        nc.gpsimd.memset(w2_plane[:].bitcast(U32), 0)
 
         def load_scale_rows(queue, q):
             queue.dma_start(w2_plane[32 * q : 32 * q + 4, :].bitcast(I32), w2_scales[0, 4 * q : 4 * q + 4, :].bitcast(I32))
@@ -189,21 +190,29 @@ def tile_list_hboth_m_silu_kernel(tc, xT, w1, w2_words, w2_scales, wgt, b, wgo, 
             round_w1(nc.scalar.copy, 0, u)
         for t in range(2):
             quantize_w1(0, t)
-        round_w1(nc.vector.tensor_copy, 1, 0)
-        round_w1(nc.scalar.copy, 1, 1)
+        for u in range(2):
+            for q, copy in enumerate((nc.vector.tensor_copy, nc.scalar.copy)):
+                copy(
+                    w1_last_bf[u, q][:].rearrange("p t m j -> p m j t"),
+                    w1_raw[1].rearrange("p j (m t) -> p m j t", t=PACK)[:, q * M_QUARTER : (q + 1) * M_QUARTER, :, 2 * u : 2 * u + 2],
+                )
         round_xg(nc.scalar.copy, xg_late[:, :CHUNK, :], HALF, HALF + CHUNK, 0)
-        for t in range(2, PACK):
-            quantize_w1(0, t)
         for t in range(PACK):
-            quantize_w1(1, t)
+            if t >= 2:
+                quantize_w1(0, t)
+            for q in range(2):
+                ms = slice(M_HALF + q * M_QUARTER, M_HALF + (q + 1) * M_QUARTER)
+                nc.vector.quantize_mx(w1_codes[:, t, ms].bitcast(FP8X4), w1_scales[:, t, ms], w1_last_bf[t // 2, q][:, t % 2].rearrange("p m j -> p (m j)"))
+        xg1 = quantize(xg_bf[1], CHUNK, "xg1", tag="w1_last_bf00")
 
         h_bf = [mx_tile([P, CHUNK, PACK], BF16, f"h_bf{c}") for c in range(2)]
         for u in range(2):
             relu(h_bf[0][:, :, 2 * u : 2 * u + 2], layer1(xg0, f"h_ps0{u}", 0, range(2 * u, 2 * u + 2)))
-        gather(PACK - 1, HALF, S)
-        xg1 = quantize(xg_bf[1], CHUNK, "xg1", scales=w1_scales[4:, PACK - 1, :])
+        for c in range(2, 4):
+            gather(PACK - 1, c * CHUNK, (c + 1) * CHUNK)
         relu(h_bf[1][:], layer1(xg1, "h_ps1"))
-        round_xg(nc.vector.tensor_copy, xg_late, HALF, S, 1)
+        for c in range(2):
+            round_xg(nc.vector.tensor_copy, xg_late[:, c * CHUNK : (c + 1) * CHUNK, :], HALF + c * CHUNK, HALF + (c + 1) * CHUNK, 1)
 
         h0 = quantize(h_bf[0][:], CHUNK, "h0")
         for blk in range(2):

@@ -186,6 +186,27 @@ def tile_list_hboth_m_silu_kernel(tc, xT, w1, w2_words, w2_scales, wgt, b, wgo, 
         for c in range(2):
             round_xg(nc.vector.tensor_copy, xg_bf[c], c * CHUNK, (c + 1) * CHUNK, 1)
         xg0 = quantize(xg_bf[0], CHUNK, "xg0")
+        warm_ps = ps.tile([BLOCK, PACK, CHUNK], F32, name="warm_ps", tag="y_ps1")
+        for k in range(PACK):
+            nc.tensor.matmul_mx(
+                warm_ps[:, k, :],
+                lhsT=xg0[0][:, :BLOCK].bitcast(FP8X4),
+                lhsT_scale=xg0[1][:, :BLOCK],
+                rhs=xg0[0][:].bitcast(FP8X4),
+                rhs_scale=xg0[1],
+                start=True,
+                stop=True,
+            )
+        warm_wide = ps.tile([P, CHUNK], F32, name="warm_wide", tag="y_ps01")
+        nc.tensor.matmul_mx(
+            warm_wide[:],
+            lhsT=xg0[0][:].bitcast(FP8X4),
+            lhsT_scale=xg0[1],
+            rhs=xg0[0][:].bitcast(FP8X4),
+            rhs_scale=xg0[1],
+            start=True,
+            stop=True,
+        )
         for u in range(2):
             round_w1(nc.scalar.copy, 0, u)
         for t in range(2):

@@ -60,12 +60,12 @@ def tile_list_hboth_m_silu_kernel(tc, xT, w1, w2_words, w2_scales, wgt, b, wgo, 
         xg_late = shared[:, raw_end - HALF :].bitcast(BF16).rearrange("p (n i) -> p n i", i=PACK)
         xg_bf = [mx_tile([P, CHUNK, PACK], BF16, f"xg_bf{c}")[:] for c in range(2)]
         warm_in = sb.tile([P, 1], F32, name="warm_in")
-        warm_out = sb.tile([P, 1], F32, name="warm_out")
+        zero = shared[:, raw_end + HALF - 1 :]
 
         w2_plane = mx_tile([P, M], U8, "w2_plane")
         nc.vector.memset(w2_plane[:].bitcast(U32), 0)
         nc.vector.memset(warm_in[:], 0.0)
-        nc.scalar.activation(warm_out[:], warm_in[:], ACT.Silu)
+        nc.scalar.activation(zero, warm_in[:], ACT.Silu)
         nc.vector.memset(window[0][:], 0.0)
 
         x_rows = xT.rearrange("(p i) t -> p i t", i=PACK)
@@ -102,6 +102,14 @@ def tile_list_hboth_m_silu_kernel(tc, xT, w1, w2_words, w2_scales, wgt, b, wgo, 
             nc.vector.quantize_mx(codes[:].bitcast(FP8X4), scales, src.rearrange("p n i -> p (n i)"))
             return codes, scales
 
+        def quantize_chunks(src, name, tag):
+            codes = mx_tile([P, HALF], U32, name + "_codes", tag)
+            scales = mx_tile([P, HALF], U8, name + "_scales")[:]
+            for c in range(2):
+                cols = slice(c * CHUNK, (c + 1) * CHUNK)
+                nc.vector.quantize_mx(codes[:, cols].bitcast(FP8X4), scales[:, cols], src[:, cols, :].rearrange("p n i -> p (n i)"))
+            return codes, scales
+
         def round_w1(copy, h, u):
             copy(
                 w1_bf[u][:, :, h * M_HALF : (h + 1) * M_HALF, :].rearrange("p t m j -> p m j t"),
@@ -123,8 +131,8 @@ def tile_list_hboth_m_silu_kernel(tc, xT, w1, w2_words, w2_scales, wgt, b, wgo, 
                 )
             return h_ps
 
-        def relu(dst, h_ps):
-            nc.scalar.activation(dst, h_ps[:].rearrange("p t n -> p n t"), ACT.Relu, bias=warm_out[:])
+        def relu(dst, h_ps, bias=0.0):
+            nc.scalar.activation(dst, h_ps[:].rearrange("p t n -> p n t"), ACT.Relu, bias=bias)
 
         def layer2(dst, operand, blk):
             codes, scales = operand
@@ -217,7 +225,6 @@ def tile_list_hboth_m_silu_kernel(tc, xT, w1, w2_words, w2_scales, wgt, b, wgo, 
                     w1_last_bf[u, q][:].rearrange("p t m j -> p m j t"),
                     w1_raw[1].rearrange("p j (m t) -> p m j t", t=PACK)[:, q * M_QUARTER : (q + 1) * M_QUARTER, :, 2 * u : 2 * u + 2],
                 )
-        round_xg(nc.scalar.copy, xg_late[:, :CHUNK, :], HALF, HALF + CHUNK, 0)
         for t in range(PACK):
             if t >= 2:
                 quantize_w1(0, t)
@@ -228,19 +235,22 @@ def tile_list_hboth_m_silu_kernel(tc, xT, w1, w2_words, w2_scales, wgt, b, wgo, 
 
         h_bf = [mx_tile([P, CHUNK, PACK], BF16, f"h_bf{c}") for c in range(2)]
         for u in range(2):
-            relu(h_bf[0][:, :, 2 * u : 2 * u + 2], layer1(xg0, f"h_ps0{u}", 0, range(2 * u, 2 * u + 2)))
+            relu(h_bf[0][:, :, 2 * u : 2 * u + 2], layer1(xg0, f"h_ps0{u}", 0, range(2 * u, 2 * u + 2)), zero)
         for c in range(2, 4):
             gather(PACK - 1, c * CHUNK, (c + 1) * CHUNK)
         relu(h_bf[1][:], layer1(xg1, "h_ps1"))
-        for c in range(2):
-            round_xg(nc.vector.tensor_copy, xg_late[:, c * CHUNK : (c + 1) * CHUNK, :], HALF + c * CHUNK, HALF + (c + 1) * CHUNK, 1)
+        nc.vector.tensor_copy(
+            xg_late[:, :CHUNK, :].rearrange("p (c n) i -> p c i n", n=4),
+            picked[:, :, HALF : HALF + CHUNK].rearrange("p i (c n) -> p c i n", n=4),
+        )
 
         h0 = quantize(h_bf[0][:], CHUNK, "h0")
+        round_xg(nc.vector.tensor_copy, xg_late[:, CHUNK:, :], S - CHUNK, S, 1)
         for blk in range(2):
             y_ps = ps.tile([P, CHUNK], F32, name=f"y_ps0{blk}")
             layer2(y_ps[:], h0, blk)
             silu(y_ps[:], blk, 0, CHUNK)
-        xg2 = quantize(xg_late, HALF, "xg2", tag="h_bf0")
+        xg2 = quantize_chunks(xg_late, "xg2", "h_bf0")
         h1 = quantize(h_bf[1][:], CHUNK, "h1")
         for blk in range(2):
             scatter(blk, 0, CHUNK)
@@ -252,10 +262,7 @@ def tile_list_hboth_m_silu_kernel(tc, xT, w1, w2_words, w2_scales, wgt, b, wgo, 
             layer2(y_ps1[:, blk, :], h1, blk)
         for blk in range(2):
             silu(y_ps1[:, blk, :], blk, CHUNK, HALF)
-        h2 = mx_tile([P, HALF], U32, "h2_codes", "y_sb0_0"), mx_tile([P, HALF], U8, "h2_scales")[:]
-        for c in range(2):
-            cols = slice(c * CHUNK, (c + 1) * CHUNK)
-            nc.vector.quantize_mx(h2[0][:, cols].bitcast(FP8X4), h2[1][:, cols], h_bf2[:, cols, :].rearrange("p n i -> p (n i)"))
+        h2 = quantize_chunks(h_bf2, "h2", "y_sb0_0")
         for blk in range(2):
             scatter(blk, CHUNK, HALF)
         for blk in range(2):

@@ -92,6 +92,12 @@ def tile_list_hboth_m_silu_kernel(tc, xT, w1, w2_words, w2_scales, wgt, b, wgo, 
                 picked[:, 2 * u : 2 * u + 2, lo:hi].rearrange("p i (c n) -> p c i n", n=4),
             )
 
+        def round_late(c):
+            nc.vector.tensor_copy(
+                xg_late[:, c * CHUNK : (c + 1) * CHUNK, :].rearrange("p (c n) i -> p c i n", n=4),
+                picked[:, :, HALF + c * CHUNK : HALF + (c + 1) * CHUNK].rearrange("p i (c n) -> p c i n", n=4),
+            )
+
         def quantize_w1(h, t):
             ms = slice(h * M_HALF, (h + 1) * M_HALF)
             nc.vector.quantize_mx(w1_codes[:, t, ms].bitcast(FP8X4), w1_scales[:, t, ms], w1_bf[t // 2][:, t % 2, ms, :].rearrange("p m j -> p (m j)"))
@@ -187,7 +193,6 @@ def tile_list_hboth_m_silu_kernel(tc, xT, w1, w2_words, w2_scales, wgt, b, wgo, 
         gather(1, 0, S)
         for c in range(2):
             round_xg(nc.scalar.copy, xg_bf[c], c * CHUNK, (c + 1) * CHUNK, 0)
-        round_xg(nc.scalar.copy, xg_late[:, CHUNK:, :], S - CHUNK, S, 0)
         gather(2, 0, S)
         for c in range(2):
             gather(PACK - 1, c * CHUNK, (c + 1) * CHUNK)
@@ -239,13 +244,10 @@ def tile_list_hboth_m_silu_kernel(tc, xT, w1, w2_words, w2_scales, wgt, b, wgo, 
         for c in range(2, 4):
             gather(PACK - 1, c * CHUNK, (c + 1) * CHUNK)
         relu(h_bf[1][:], layer1(xg1, "h_ps1"))
-        nc.vector.tensor_copy(
-            xg_late[:, :CHUNK, :].rearrange("p (c n) i -> p c i n", n=4),
-            picked[:, :, HALF : HALF + CHUNK].rearrange("p i (c n) -> p c i n", n=4),
-        )
+        round_late(0)
 
         h0 = quantize(h_bf[0][:], CHUNK, "h0")
-        round_xg(nc.vector.tensor_copy, xg_late[:, CHUNK:, :], S - CHUNK, S, 1)
+        round_late(1)
         for blk in range(2):
             y_ps = ps.tile([P, CHUNK], F32, name=f"y_ps0{blk}")
             layer2(y_ps[:], h0, blk)

@@ -41,7 +41,6 @@ def tile_list_hboth_m_silu_kernel(tc, xT, w1, w2_words, w2_scales, wgt, b, wgo, 
         wgt_rows = mx_tile([P, BLOCK], F32, "wgt_rows")
         wgt_turned = mx_tile([P, BLOCK], F32, "wgt_turned")
         wgt_spread = mx_tile([P, S], F32, "wgt_spread")
-        wgt_sb = mx_tile([P, S], F32, "wgt_sb")
         wgo_sb = sb.tile([P, S], F32, name="wgo_sb")
         x_plane = [mx_tile([P, T], F32, f"x_plane{i}") for i in range(PACK)]
         w1_bf = [mx_tile([P, 2, M_HALF, PACK], BF16, f"w1_bf{u}") for u in range(2)]
@@ -52,10 +51,12 @@ def tile_list_hboth_m_silu_kernel(tc, xT, w1, w2_words, w2_scales, wgt, b, wgo, 
         bias = sb.tile([P, M // P], F32, name="bias")
         window = [sb.tile([P, T], F32, name="window0")]
         w1_first = sb.tile([P, PACK, W_HALF], F32, name="w1_first")
-        raw_end = PACK * S - HALF + PACK * W_HALF
+        raw_start = (PACK - 1) * T + HALF
+        raw_end = raw_start + PACK * W_HALF
         shared = mx_tile([P, raw_end + HALF], F32, "shared")
-        picked = shared[:, : PACK * S].rearrange("p (i s) -> p i s", i=PACK)
-        w1_raw = [w1_first[:], shared[:, PACK * S - HALF : raw_end].rearrange("p (j c) -> p j c", j=PACK)]
+        picked = shared[:, : PACK * T].rearrange("p (i s) -> p i s", i=PACK)[:, :, :S]
+        wgt_sb = shared[:, 2 * T + S - CHUNK : 2 * T + 2 * S - CHUNK]
+        w1_raw = [w1_first[:], shared[:, raw_start:raw_end].rearrange("p (j c) -> p j c", j=PACK)]
         y_sb = {(blk, lo): mx_tile([P, hi - lo], F32, f"y_sb{blk}_{lo}") for blk in range(2) for lo, hi in ((0, CHUNK), (CHUNK, HALF), (HALF, S))}
         xg_late = shared[:, raw_end - HALF :].bitcast(BF16).rearrange("p (n i) -> p n i", i=PACK)
         xg_bf = [mx_tile([P, CHUNK, PACK], BF16, f"xg_bf{c}")[:] for c in range(2)]
@@ -67,6 +68,10 @@ def tile_list_hboth_m_silu_kernel(tc, xT, w1, w2_words, w2_scales, wgt, b, wgo, 
         nc.vector.memset(warm_in[:], 0.0)
         nc.scalar.activation(zero, warm_in[:], ACT.Silu)
         nc.vector.memset(window[0][:], 0.0)
+        xg0_codes = mx_tile([P, S], U32, "xg0_codes")
+        xg0_scales = mx_tile([P, S], U8, "xg0_scales")
+        nc.vector.memset(xg0_codes[:, CHUNK:], 0)
+        nc.vector.memset(xg0_scales[:, CHUNK:].bitcast(U32), 0)
 
         x_rows = xT.rearrange("(p i) t -> p i t", i=PACK)
         w1_rows = w1.rearrange("(p j) c -> p j c", j=PACK)
@@ -193,33 +198,25 @@ def tile_list_hboth_m_silu_kernel(tc, xT, w1, w2_words, w2_scales, wgt, b, wgo, 
         gather(1, 0, S)
         for c in range(2):
             round_xg(nc.scalar.copy, xg_bf[c], c * CHUNK, (c + 1) * CHUNK, 0)
-        gather(2, 0, S)
+        gather(2, 0, HALF)
         for c in range(2):
             gather(PACK - 1, c * CHUNK, (c + 1) * CHUNK)
-        for c in range(2):
-            round_xg(nc.vector.tensor_copy, xg_bf[c], c * CHUNK, (c + 1) * CHUNK, 1)
-        xg0 = quantize(xg_bf[0], CHUNK, "xg0")
-        warm_ps = ps.tile([BLOCK, PACK, CHUNK], F32, name="warm_ps", tag="y_ps1")
-        for k in range(PACK):
+        round_xg(nc.vector.tensor_copy, xg_bf[0], 0, CHUNK, 1)
+        xg0 = (xg0_codes, xg0_scales[:])
+        nc.vector.quantize_mx(xg0_codes[:, :CHUNK].bitcast(FP8X4), xg0_scales[:, :CHUNK], xg_bf[0].rearrange("p n i -> p (n i)"))
+        round_xg(nc.vector.tensor_copy, xg_bf[1], CHUNK, HALF, 1)
+        gather(2, HALF, S)
+        for bank in ("y_ps1", "y_ps01"):
+            warm_ps = ps.tile([BLOCK, S], F32, name="warm_" + bank, tag=bank)
             nc.tensor.matmul_mx(
-                warm_ps[:, k, :],
-                lhsT=xg0[0][:, :BLOCK].bitcast(FP8X4),
-                lhsT_scale=xg0[1][:, :BLOCK],
-                rhs=xg0[0][:].bitcast(FP8X4),
-                rhs_scale=xg0[1],
+                warm_ps[:],
+                lhsT=xg0_codes[:, :BLOCK].bitcast(FP8X4),
+                lhsT_scale=xg0_scales[:, :BLOCK],
+                rhs=xg0_codes[:].bitcast(FP8X4),
+                rhs_scale=xg0_scales[:],
                 start=True,
                 stop=True,
             )
-        warm_wide = ps.tile([P, CHUNK], F32, name="warm_wide", tag="y_ps01")
-        nc.tensor.matmul_mx(
-            warm_wide[:],
-            lhsT=xg0[0][:].bitcast(FP8X4),
-            lhsT_scale=xg0[1],
-            rhs=xg0[0][:].bitcast(FP8X4),
-            rhs_scale=xg0[1],
-            start=True,
-            stop=True,
-        )
         for u in range(2):
             round_w1(nc.scalar.copy, 0, u)
         for t in range(2):

from contextlib import ExitStack

import concourse.mybir as mybir

K, H, M, T, S = 512, 512, 256, 1024, 512
FLOPS = 2 * K * H * S + 2 * H * M * S

F32 = mybir.dt.float32
BF16 = mybir.dt.bfloat16
I32 = mybir.dt.int32
U32 = mybir.dt.uint32
U16 = mybir.dt.uint16
U8 = mybir.dt.uint8
FP8X4 = mybir.dt.float8_e4m3fn_x4
FP4X4 = mybir.dt.float4_e2m1fn_x4
MULT = mybir.AluOpType.mult
ACT = mybir.ActivationFunctionType

P = 128
PACK = 4
GROUP = 16
HALF = S // 2
CHUNK = 128
W_HALF = H // 2
M_HALF = W_HALF // PACK
M_QUARTER = M_HALF // 2
BLOCK = 32


def tile_list_hboth_m_silu_kernel(tc, xT, w1, w2_words, w2_scales, wgt, b, wgo, offs, offs2, out):
    nc = tc.nc
    with ExitStack() as ctx:
        sb = ctx.enter_context(tc.tile_pool(name="sb", bufs=1))
        ps = ctx.enter_context(tc.psum_pool(name="ps", bufs=1))

        def mx_tile(shape, dtype, name, tag=None):
            return sb.tile(shape, dtype, name=name, tag=tag or name, align_bytes=64)

        gather_list = sb.tile([P, S // GROUP], U16, name="gather_list")
        scatter_list = sb.tile([P, S // GROUP], U16, name="scatter_list")
        wgt_rows = mx_tile([P, BLOCK], F32, "wgt_rows")
        wgt_turned = mx_tile([P, BLOCK], F32, "wgt_turned")
        wgt_spread = mx_tile([P, S], F32, "wgt_spread")
        wgo_sb = sb.tile([P, S], F32, name="wgo_sb")
        x_plane = [mx_tile([P, T], F32, f"x_plane{i}") for i in range(PACK)]
        w1_bf = [mx_tile([P, 2, M_HALF, PACK], BF16, f"w1_bf{u}") for u in range(2)]
        w1_last_bf = {(u, q): mx_tile([P, 2, M_QUARTER, PACK], BF16, f"w1_last_bf{u}{q}") for u in range(2) for q in range(2)}
        w1_codes = mx_tile([P, PACK, P], U32, "w1_codes")
        w1_scales = mx_tile([P, PACK, P], U8, "w1_scales")
        w2_codes = mx_tile([P, 2 * M], U8, "w2_codes")
        bias = sb.tile([P, M // P], F32, name="bias")
        window = [sb.tile([P, T], F32, name="window0")]
        w1_first = sb.tile([P, PACK, W_HALF], F32, name="w1_first")
        raw_start = (PACK - 1) * T + HALF
        raw_end = raw_start + PACK * W_HALF
        shared = mx_tile([P, raw_end + HALF], F32, "shared")
        picked = shared[:, : PACK * T].rearrange("p (i s) -> p i s", i=PACK)[:, :, :S]
        wgt_sb = shared[:, 2 * T + S - CHUNK : 2 * T + 2 * S - CHUNK]
        w1_raw = [w1_first[:], shared[:, raw_start:raw_end].rearrange("p (j c) -> p j c", j=PACK)]
        y_sb = {(blk, lo): mx_tile([P, hi - lo], F32, f"y_sb{blk}_{lo}") for blk in range(2) for lo, hi in ((0, CHUNK), (CHUNK, HALF), (HALF, S))}
        xg_late = shared[:, raw_end - HALF :].bitcast(BF16).rearrange("p (n i) -> p n i", i=PACK)
        xg_bf = [mx_tile([P, CHUNK, PACK], BF16, f"xg_bf{c}")[:] for c in range(2)]
        warm_in = sb.tile([P, 1], F32, name="warm_in")
        zero = shared[:, raw_end + HALF - 1 :]

        w2_plane = mx_tile([P, M], U8, "w2_plane")
        nc.vector.memset(w2_plane[:].bitcast(U32), 0)
        nc.vector.memset(warm_in[:], 0.0)
        nc.scalar.activation(zero, warm_in[:], ACT.Silu)
        nc.vector.memset(window[0][:], 0.0)
        xg0_codes = mx_tile([P, S], U32, "xg0_codes")
        xg0_scales = mx_tile([P, S], U8, "xg0_scales")
        nc.vector.memset(xg0_codes[:, CHUNK:], 0)
        nc.vector.memset(xg0_scales[:, CHUNK:].bitcast(U32), 0)

        x_rows = xT.rearrange("(p i) t -> p i t", i=PACK)
        w1_rows = w1.rearrange("(p j) c -> p j c", j=PACK)
        nc.sync.dma_start(wgt_rows[:], wgt.rearrange("p (a c) -> (p a) c", c=HALF)[:: GROUP + 1, :].rearrange("u (n c) -> u n c", c=BLOCK))
        nc.sync.dma_start(x_plane[0][:], x_rows[:, 0, :])
        nc.sync.dma_start(gather_list[:], offs)
        for i in range(1, PACK):
            nc.sync.dma_start(x_plane[i][:], x_rows[:, i, :])
        for h in range(2):
            nc.sync.dma_start(w1_raw[h], w1_rows[:, :, h * W_HALF : (h + 1) * W_HALF])

        def gather(i, lo, hi):
            nc.vector.tensor_tensor(
                picked[:, i, lo:hi],
                x_plane[i][:].indirect(gather_list[:, lo // GROUP : hi // GROUP]),
                wgt_sb[:, lo:hi],
                MULT,
            )

        def round_xg(copy, dst, lo, hi, u):
            copy(
                dst[:, :, 2 * u : 2 * u + 2].rearrange("p (c n) i -> p c i n", n=4),
                picked[:, 2 * u : 2 * u + 2, lo:hi].rearrange("p i (c n) -> p c i n", n=4),
            )

        def round_late(c):
            nc.vector.tensor_copy(
                xg_late[:, c * CHUNK : (c + 1) * CHUNK, :].rearrange("p (c n) i -> p c i n", n=4),
                picked[:, :, HALF + c * CHUNK : HALF + (c + 1) * CHUNK].rearrange("p i (c n) -> p c i n", n=4),
            )

        def quantize_w1(h, t):
            ms = slice(h * M_HALF, (h + 1) * M_HALF)
            nc.vector.quantize_mx(w1_codes[:, t, ms].bitcast(FP8X4), w1_scales[:, t, ms], w1_bf[t // 2][:, t % 2, ms, :].rearrange("p m j -> p (m j)"))

        def quantize(src, width, name, tag=None):
            codes = mx_tile([P, width], U32, name + "_codes", tag)
            scales = mx_tile([P, width], U8, name + "_scales")[:]
            nc.vector.quantize_mx(codes[:].bitcast(FP8X4), scales, src.rearrange("p n i -> p (n i)"))
            return codes, scales

        def quantize_chunks(src, name, tag):
            codes = mx_tile([P, HALF], U32, name + "_codes", tag)
            scales = mx_tile([P, HALF], U8, name + "_scales")[:]
            for c in range(2):
                cols = slice(c * CHUNK, (c + 1) * CHUNK)
                nc.vector.quantize_mx(codes[:, cols].bitcast(FP8X4), scales[:, cols], src[:, cols, :].rearrange("p n i -> p (n i)"))
            return codes, scales

        def round_w1(copy, h, u):
            copy(
                w1_bf[u][:, :, h * M_HALF : (h + 1) * M_HALF, :].rearrange("p t m j -> p m j t"),
                w1_raw[h].rearrange("p j (m t) -> p m j t", t=PACK)[:, :, :, 2 * u : 2 * u + 2],
            )

        def layer1(operand, name, lo=0, slices=range(PACK)):
            codes, scales = operand
            h_ps = ps.tile([P, len(slices), CHUNK], F32, name=name)
            for k, t in enumerate(slices):
                nc.tensor.matmul_mx(
                    h_ps[:, k, :],
                    lhsT=w1_codes[:, t, :].bitcast(FP8X4),
                    lhsT_scale=w1_scales[:, t, :],
                    rhs=codes[:, lo : lo + CHUNK].bitcast(FP8X4),
                    rhs_scale=scales[:, lo : lo + CHUNK],
                    start=True,
                    stop=True,
                )
            return h_ps

        def relu(dst, h_ps, bias=0.0):
            nc.scalar.activation(dst, h_ps[:].rearrange("p t n -> p n t"), ACT.Relu, bias=bias)

        def layer2(dst, operand, blk):
            codes, scales = operand
            nc.tensor.matmul_mx(
                dst,
                lhsT=w2_codes[:, 2 * blk * P : 2 * (blk + 1) * P].bitcast(FP4X4),
                lhsT_scale=w2_plane[:, blk * P : (blk + 1) * P],
                rhs=codes[:].bitcast(FP8X4),
                rhs_scale=scales,
                start=True,
                stop=True,
            )

        def silu(y_ps, blk, lo, hi):
            nc.scalar.activation(y_sb[blk, lo][:], y_ps, ACT.Silu, bias=bias[:, blk : blk + 1])

        def scatter(blk, lo, hi):
            nc.vector.tensor_tensor(
                window[blk][:].indirect(scatter_list[:, lo // GROUP : hi // GROUP]),
                y_sb[blk, lo][:],
                wgo_sb[:, lo:hi],
                MULT,
            )

        nc.vector.transpose(wgt_turned[:], wgt_rows[:])
        blocks = HALF // BLOCK
        for a in range(2):
            nc.vector.tensor_copy(
                wgt_spread[:, a * HALF : (a + 1) * HALF].rearrange("p (n g r) -> p n g r", g=2, r=GROUP),
                wgt_turned[:].rearrange("p (g n) -> p n g", g=2)[:, a * blocks : (a + 1) * blocks, :].unsqueeze(3).to_broadcast([P, blocks, 2, GROUP]),
            )
        for a in range(2):
            nc.vector.transpose(wgt_sb[:, a * HALF : (a + 1) * HALF], wgt_spread[:, a * HALF : (a + 1) * HALF])

        def load_scale_rows(queue, q):
            queue.dma_start(w2_plane[32 * q : 32 * q + 4, :].bitcast(I32), w2_scales[0, 4 * q : 4 * q + 4, :].bitcast(I32))

        for q in range(2):
            load_scale_rows(nc.gpsimd, q)
        for q in range(2, 4):
            load_scale_rows(nc.sync, q)
        nc.sync.dma_start(w2_codes[:].bitcast(I32), w2_words[0].bitcast(I32))
        with nc.allow_non_contiguous_dma(reason="one bias value a partition"):
            nc.sync.dma_start(bias[:], b.rearrange("(c p) -> p c", p=P))
        nc.sync.dma_start(wgo_sb[:], wgo)
        nc.sync.dma_start(scatter_list[:], offs2)

        window.append(mx_tile([P, T], F32, "window1", "wgt_spread"))
        nc.gpsimd.memset(window[1][:], 0.0)
        for a in range(2):
            gather(0, a * HALF, (a + 1) * HALF)
        gather(1, 0, S)
        for c in range(2):
            round_xg(nc.scalar.copy, xg_bf[c], c * CHUNK, (c + 1) * CHUNK, 0)
        gather(2, 0, HALF)
        for c in range(2):
            gather(PACK - 1, c * CHUNK, (c + 1) * CHUNK)
        round_xg(nc.vector.tensor_copy, xg_bf[0], 0, CHUNK, 1)
        xg0 = (xg0_codes, xg0_scales[:])
        nc.vector.quantize_mx(xg0_codes[:, :CHUNK].bitcast(FP8X4), xg0_scales[:, :CHUNK], xg_bf[0].rearrange("p n i -> p (n i)"))
        round_xg(nc.vector.tensor_copy, xg_bf[1], CHUNK, HALF, 1)
        gather(2, HALF, S)
        for bank in ("y_ps1", "y_ps01"):
            warm_ps = ps.tile([BLOCK, S], F32, name="warm_" + bank, tag=bank)
            nc.tensor.matmul_mx(
                warm_ps[:],
                lhsT=xg0_codes[:, :BLOCK].bitcast(FP8X4),
                lhsT_scale=xg0_scales[:, :BLOCK],
                rhs=xg0_codes[:].bitcast(FP8X4),
                rhs_scale=xg0_scales[:],
                start=True,
                stop=True,
            )
        for u in range(2):
            round_w1(nc.scalar.copy, 0, u)
        for t in range(2):
            quantize_w1(0, t)
        for u in range(2):
            for q, copy in enumerate((nc.vector.tensor_copy, nc.scalar.copy)):
                copy(
                    w1_last_bf[u, q][:].rearrange("p t m j -> p m j t"),
                    w1_raw[1].rearrange("p j (m t) -> p m j t", t=PACK)[:, q * M_QUARTER : (q + 1) * M_QUARTER, :, 2 * u : 2 * u + 2],
                )
        for t in range(PACK):
            if t >= 2:
                quantize_w1(0, t)
            for q in range(2):
                ms = slice(M_HALF + q * M_QUARTER, M_HALF + (q + 1) * M_QUARTER)
                nc.vector.quantize_mx(w1_codes[:, t, ms].bitcast(FP8X4), w1_scales[:, t, ms], w1_last_bf[t // 2, q][:, t % 2].rearrange("p m j -> p (m j)"))
        xg1 = quantize(xg_bf[1], CHUNK, "xg1", tag="w1_last_bf00")

        h_bf = [mx_tile([P, CHUNK, PACK], BF16, f"h_bf{c}") for c in range(2)]
        for u in range(2):
            relu(h_bf[0][:, :, 2 * u : 2 * u + 2], layer1(xg0, f"h_ps0{u}", 0, range(2 * u, 2 * u + 2)), zero)
        for c in range(2, 4):
            gather(PACK - 1, c * CHUNK, (c + 1) * CHUNK)
        relu(h_bf[1][:], layer1(xg1, "h_ps1"))
        round_late(0)

        h0 = quantize(h_bf[0][:], CHUNK, "h0")
        round_late(1)
        for blk in range(2):
            y_ps = ps.tile([P, CHUNK], F32, name=f"y_ps0{blk}")
            layer2(y_ps[:], h0, blk)
            silu(y_ps[:], blk, 0, CHUNK)
        xg2 = quantize_chunks(xg_late, "xg2", "h_bf0")
        h1 = quantize(h_bf[1][:], CHUNK, "h1")
        for blk in range(2):
            scatter(blk, 0, CHUNK)
        h_bf2 = mx_tile([P, HALF, PACK], BF16, "h_bf2", "h0_codes")
        for c in range(2):
            relu(h_bf2[:, c * CHUNK : (c + 1) * CHUNK, :], layer1(xg2, f"h_ps{2 + c}", c * CHUNK))
        y_ps1 = ps.tile([P, 2, CHUNK], F32, name="y_ps1")
        for blk in range(2):
            layer2(y_ps1[:, blk, :], h1, blk)
        for blk in range(2):
            silu(y_ps1[:, blk, :], blk, CHUNK, HALF)
        h2 = quantize_chunks(h_bf2, "h2", "y_sb0_0")
        for blk in range(2):
            scatter(blk, CHUNK, HALF)
        for blk in range(2):
            y_ps2 = ps.tile([P, HALF], F32, name=f"y_ps2{blk}", tag=f"h_ps0{blk}")
            layer2(y_ps2[:], h2, blk)
            silu(y_ps2[:], blk, HALF, S)
            scatter(blk, HALF, S)
            nc.sync.dma_start(out[blk * P : (blk + 1) * P, :], window[blk][:])
